import numpy as np
import ml_dtypes


def mxq(x, axis, fmt="e4m3"):
    dtype, down = {"e4m3": (ml_dtypes.float8_e4m3fn, 7), "e5m2": (ml_dtypes.float8_e5m2, 14)}[fmt]
    v = np.moveaxis(np.asarray(x, np.float32).astype(ml_dtypes.bfloat16).astype(np.float64), axis, -1)
    blocks = v.reshape(v.shape[:-1] + (-1, 32))
    amax = np.abs(blocks).max(-1, keepdims=True)
    byte = np.maximum(np.where(amax > 0, np.frexp(amax)[1] - 1 + 127, 0) - down, 1)
    scale = np.exp2(byte - 127.0)
    codes = (blocks / scale).astype(np.float32).astype(dtype).astype(np.float64)
    return np.moveaxis((codes * scale).reshape(v.shape), -1, axis)


WIDE = False


def mx_kscale(k):
    if not WIDE:
        return np.ones(k)
    levels = np.array([10, -10, 5, -5, 0])
    if k % 512:
        return np.exp2(np.random.permutation(np.resize(levels, k // 32))).repeat(32)
    a = np.empty((k // 512, 16))
    for p in range(k // 512):
        a[p, :8] = np.random.permutation(np.resize(levels, 8))
        for g in range(8):
            far = levels[np.abs(levels - a[p, g]) >= 10]
            a[p, g + 8] = far[np.random.randint(len(far))]
    return np.exp2(a.ravel()).repeat(32)


def f64(x):
    return np.asarray(x).astype(np.float64)


def striped(idx):
    return np.tile(idx.reshape(-1, 16).T, (8, 1)).astype(np.uint16)


def unstriped(offs):
    return offs[:16].T.reshape(-1).astype(np.int64)


E2M1 = np.array([0.0, 0.5, 1.0, 1.5, 2.0, 3.0, 4.0, 6.0, -0.0, -0.5, -1.0, -1.5, -2.0, -3.0, -4.0, -6.0])


def pack_weight(w, fmt):
    k, n = w.shape
    w = f64(np.asarray(w, np.float32).astype(ml_dtypes.bfloat16)).reshape(k // 32, 32, n)
    amax = np.abs(w).max(1)
    if fmt == "e4m3":
        byte = np.frexp(amax)[1] - 1 + 127 - 7
    else:
        mant, ex = np.frexp(amax / 6.0)
        byte = np.where(mant > 0.5, ex, ex - 1) + 127
    byte = np.clip(np.where(amax > 0, byte, 1), 1, 254)
    scaled = (w * np.exp2(127.0 - byte)[:, None, :]).reshape(k, n).astype(np.float32)
    by_word = np.ascontiguousarray(scaled.reshape(k // 512, 128, 4, n).transpose(0, 1, 3, 2))
    if fmt == "e4m3":
        words = by_word.astype(ml_dtypes.float8_e4m3fn).view(np.uint8)
    else:
        c = by_word.astype(ml_dtypes.float4_e2m1fn).view(np.uint8) & 0xF
        words = (c[..., 0::2] | (c[..., 1::2] << 4)).reshape(k // 512, 128, 2 * n)
    return np.ascontiguousarray(words), np.ascontiguousarray(byte.astype(np.uint8).reshape(k // 512, 16, n))


def unpack_weight(words, scales, fmt):
    g, _, n = scales.shape
    words = np.ascontiguousarray(words).reshape(g, 128, n, -1)
    if fmt == "e4m3":
        vals = words.view(ml_dtypes.float8_e4m3fn).astype(np.float64)
    else:
        nib = np.empty((g, 128, n, 4), np.uint8)
        nib[..., 0::2] = words & 0xF
        nib[..., 1::2] = words >> 4
        vals = E2M1[nib]
    vals = vals * np.repeat(np.exp2(scales.astype(np.float64) - 127.0), 8, axis=1)[..., None]
    return vals.transpose(0, 1, 3, 2).reshape(g * 512, n)


def gelu(v):
    return 0.5 * v * (1.0 + np.tanh(np.sqrt(2.0 / np.pi) * (v + 0.044715 * v**3)))


K, T, E, C, H, N = 1024, 1280, 4, 256, 512, 256


def by_expert(wq, xq):
    return np.concatenate([wq[e].T @ xq[:, e * C:(e + 1) * C] for e in range(E)], axis=1)


def setup_inputs():
    n = np.random.standard_normal
    s = mx_kscale(K)[:, None]
    u = mx_kscale(H)
    w1 = [pack_weight(m, "e2m1") for m in n((E, K, H)) / np.sqrt(K) / s[None] * u[None, None, :]]
    w2 = [pack_weight(m, "e2m1") for m in n((E, H, N)) / np.sqrt(H) / u[None, :, None]]
    x = pack_weight(n((K, T)) * s, "e4m3")
    return {
        "x_words": x[0],
        "x_scales": x[1],
        "w1_words": np.stack([m[0] for m in w1]),
        "w1_scales": np.stack([m[1] for m in w1]),
        "w2_words": np.stack([m[0] for m in w2]),
        "w2_scales": np.stack([m[1] for m in w2]),
        "gate": np.tile(np.random.uniform(0.2, 1.0, E * C), (N, 1)).astype(np.float32),
        "offs": striped(np.random.permutation(T)[:E * C]),
        "dst": striped(np.random.permutation(T)[:E * C]),
    }


def reference(x_words, x_scales, w1_words, w1_scales, w2_words, w2_scales, gate, offs, dst):
    idx = unstriped(offs)
    w1 = np.stack([unpack_weight(w1_words[e], w1_scales[e], "e2m1") for e in range(E)])
    w2 = np.stack([unpack_weight(w2_words[e], w2_scales[e], "e2m1") for e in range(E)])
    xq = unpack_weight(x_words, x_scales, "e4m3")[:, idx]
    h = gelu(by_expert(w1, xq))
    y = by_expert(w2, mxq(h, 0, "e4m3"))
    out = np.zeros((N, T))
    out[:, unstriped(dst)] = f64(gate) * y
    return out

@@ -1,0 +1,200 @@
+from contextlib import ExitStack
+
+import concourse.mybir as mybir
+from concourse.masks import make_identity
+
+K, T, E, C, H, N = 1024, 1280, 4, 256, 512, 256
+FLOPS = 2 * E * C * (K * H + H * N)
+
+F32 = mybir.dt.float32
+BF16 = mybir.dt.bfloat16
+I32 = mybir.dt.int32
+U32 = mybir.dt.uint32
+U16 = mybir.dt.uint16
+U8 = mybir.dt.uint8
+FP8X4 = mybir.dt.float8_e4m3fn_x4
+FP4X4 = mybir.dt.float4_e2m1fn_x4
+GELU = mybir.ActivationFunctionType.Gelu_apprx_tanh
+MULT = mybir.AluOpType.mult
+
+P = 128
+PASSES = K // 512
+SLOTS = E * C
+LIST_COLS = C // 16
+HALVES = N // P
+
+
+def tile_moe_two_mlp_gelu_kernel(
+    tc, x_words, x_scales, w1_words, w1_scales, w2_words, w2_scales, gate, offs, dst, out
+):
+    nc = tc.nc
+    with ExitStack() as ctx:
+        keep = ctx.enter_context(tc.tile_pool(name="keep", bufs=1))
+        work = ctx.enter_context(tc.tile_pool(name="work", bufs=2))
+        reuse = ctx.enter_context(tc.tile_pool(name="reuse", bufs=1))
+        psum_a = ctx.enter_context(tc.psum_pool(name="psum_a", bufs=3))
+        psum_t = ctx.enter_context(tc.psum_pool(name="psum_t", bufs=2))
+        psum_y = ctx.enter_context(tc.psum_pool(name="psum_y", bufs=3))
+
+        offs_sb = keep.tile([P, SLOTS // 16], U16, name="offs_sb")
+        dst_sb = keep.tile([P, SLOTS // 16], U16, name="dst_sb")
+        xs = keep.tile([P, PASSES, T], U8, name="xs", align_bytes=64)
+        xw = [keep.tile([P, T], I32, name="xw%d" % o, align_bytes=64) for o in range(PASSES)]
+        w1s = keep.tile([P, E * PASSES, H], U8, name="w1s", align_bytes=64)
+        w2s = keep.tile([P, E, N], U8, name="w2s", align_bytes=64)
+        w1w = [keep.tile([P, PASSES, 2 * H], U8, name="w1w%d" % e, align_bytes=64) for e in range(E)]
+        w2w = keep.tile([P, E, 2 * N], U8, name="w2w", align_bytes=64)
+        gate_sb = keep.tile([P, HALVES, SLOTS], F32, name="gate_sb")
+        placed = [keep.tile([P, T], F32, name="placed%d" % h) for h in range(HALVES)]
+        ident = keep.tile([P, P], F32, name="ident")
+        zero = keep.tile([P, 1], F32, name="zero")
+        warm = keep.tile([P, 1], F32, name="warm")
+
+        nc.vector.memset(xs[:].rearrange("p o t -> p (o t)").bitcast(I32), 0)
+        nc.vector.memset(w1s[:].rearrange("p g i -> p (g i)").bitcast(I32), 0)
+        nc.vector.memset(w2s[:].rearrange("p e n -> p (e n)").bitcast(I32), 0)
+        nc.gpsimd.memset(zero[:], 0.0)
+        make_identity(nc, ident[:])
+        nc.scalar.activation(warm[:], zero[:], GELU)
+        for h in range(HALVES):
+            nc.scalar.copy(placed[h][:], zero[:].to_broadcast([P, T]))
+
+        def load_w1(e):
+            nc.sync.dma_start(w1w[e][:].bitcast(I32), w1_words[e].rearrange("s p b -> p s b").bitcast(I32))
+
+        nc.sync.dma_start(offs_sb[:], offs)
+        for q in range(4):
+            nc.sync.dma_start(
+                xs[32 * q : 32 * q + 4].bitcast(I32),
+                x_scales[:, 4 * q : 4 * q + 4, :].rearrange("o f t -> f o t").bitcast(I32),
+            )
+        for o in range(PASSES):
+            nc.sync.dma_start(xw[o][:], x_words[o].rearrange("p t r -> p (t r)").bitcast(I32))
+        for q in range(4):
+            nc.sync.dma_start(
+                w1s[32 * q : 32 * q + 4].bitcast(I32),
+                w1_scales[:, :, 4 * q : 4 * q + 4, :].rearrange("e s f i -> f (e s) i").bitcast(I32),
+            )
+        load_w1(0)
+        load_w1(1)
+        for q in range(4):
+            nc.sync.dma_start(
+                w2s[32 * q : 32 * q + 4].bitcast(I32),
+                w2_scales[:, 0, 4 * q : 4 * q + 4, :].rearrange("e f n -> f e n").bitcast(I32),
+            )
+        nc.sync.dma_start(w2w[:].bitcast(I32), w2_words[:, 0].rearrange("e p b -> p e b").bitcast(I32))
+        load_w1(2)
+        load_w1(3)
+        nc.sync.dma_start(dst_sb[:], dst)
+        for h in range(HALVES):
+            nc.sync.dma_start(gate_sb[:, h, :], gate[h * P : (h + 1) * P, :])
+
+        gw = {}
+        gs = {}
+        h_cols = {}
+        y = {}
+        ysb = {}
+        H_BYTES = 2 * 4 * C
+        W_BYTES = 4 * C
+        over_words = {(2, 0): 0, (3, 0): H_BYTES}
+        over_y = {(0, 0): H_BYTES + W_BYTES, (0, 1): 2 * H_BYTES, (1, 1): 3 * H_BYTES}
+
+        def gather_scales(pair):
+            cols = offs_sb[:, 2 * pair * LIST_COLS : 2 * (pair + 1) * LIST_COLS]
+            for o in range(PASSES):
+                gs[pair, o] = keep.tile([P, 2 * C], U8, name="gs%d_%d" % (pair, o), align_bytes=64)
+                nc.vector.tensor_copy(gs[pair, o][:], xs[:, o, :].indirect(cols))
+
+        def gather_words(e, o):
+            cols = offs_sb[:, e * LIST_COLS : (e + 1) * LIST_COLS]
+            name = "gw%d_%d" % (e, o)
+            if (e, o) in over_words:
+                gw[e, o] = reuse.tile([P, C], U32, name=name, align_bytes=64, offset=over_words[e, o])
+            else:
+                gw[e, o] = keep.tile([P, C], U32, name=name, align_bytes=64)
+            nc.vector.tensor_copy(gw[e, o][:], xw[o][:].bitcast(U32).indirect(cols))
+
+        def first_layer(e):
+            turned = psum_t.tile([P, 2, C], F32, name="turned")
+            for c in range(C // P):
+                acc = psum_a.tile([P, H], F32, name="acc")
+                s0 = (e % 2) * C + c * P
+                for o in range(PASSES):
+                    nc.tensor.matmul_mx(
+                        out=acc[:],
+                        lhsT=gw[e, o][:, c * P : (c + 1) * P].bitcast(FP8X4),
+                        lhsT_scale=gs[e // 2, o][:, s0 : s0 + P],
+                        rhs=w1w[e][:, o, :].bitcast(FP4X4),
+                        rhs_scale=w1s[:, e * PASSES + o, :],
+                        start=(o == 0),
+                        stop=(o == PASSES - 1),
+                    )
+                h_rows = work.tile([P, 2, P, 2], BF16, name="h_rows", bufs=4)
+                nc.scalar.activation(h_rows[:], acc[:].rearrange("s (p u d) -> s u p d", u=2, d=2), GELU)
+                h_pairs = h_rows[:].rearrange("s u p d -> s (u p d)").bitcast(F32)
+                for u in range(2):
+                    nc.tensor.transpose(turned[:, u, c * P : (c + 1) * P], h_pairs[:, u * P : (u + 1) * P], ident[:])
+            h_cols[e] = reuse.tile([P, 4 * C], BF16, name="h_cols%d" % e, align_bytes=64, offset=e * H_BYTES)
+            nc.scalar.copy(
+                h_cols[e][:].bitcast(F32).rearrange("p (s u) -> p s u", u=2), turned[:].rearrange("p u s -> p s u")
+            )
+
+        def second_layer(e):
+            codes = work.tile([P, C], U32, name="codes", align_bytes=64)
+            h_scales = work.tile([P, C], U8, name="h_scales", align_bytes=64)
+            nc.vector.quantize_mx(out=codes[:].bitcast(FP8X4), scales=h_scales[:], in_=h_cols[e][:])
+            y[e] = psum_y.tile([P, HALVES, C], F32, name="y")
+            for h in range(HALVES):
+                nc.tensor.matmul_mx(
+                    out=y[e][:, h, :],
+                    lhsT=w2w[:, e, 2 * h * P : 2 * (h + 1) * P].bitcast(FP4X4),
+                    lhsT_scale=w2s[:, e, h * P : (h + 1) * P],
+                    rhs=codes[:].bitcast(FP8X4),
+                    rhs_scale=h_scales[:],
+                    start=True,
+                    stop=True,
+                )
+
+        def empty_y(e, h):
+            name = "ysb%d_%d" % (e, h)
+            if (e, h) in over_y:
+                ysb[e, h] = reuse.tile([P, C], F32, name=name, align_bytes=64, offset=over_y[e, h])
+            else:
+                ysb[e, h] = keep.tile([P, C], F32, name=name, align_bytes=64)
+            nc.scalar.copy(ysb[e, h][:], y[e][:, h, :])
+
+        def scatter(e, h):
+            cols = dst_sb[:, e * LIST_COLS : (e + 1) * LIST_COLS]
+            nc.vector.tensor_tensor(
+                placed[h][:].indirect(cols), ysb[e, h][:], gate_sb[:, h, e * C : (e + 1) * C], MULT
+            )
+
+        gather_scales(0)
+        for e in range(2):
+            for o in range(PASSES):
+                gather_words(e, o)
+        gather_scales(1)
+        gather_words(2, 1)
+        gather_words(3, 1)
+        first_layer(0)
+        first_layer(1)
+        second_layer(0)
+        gather_words(2, 0)
+        second_layer(1)
+        gather_words(3, 0)
+        empty_y(0, 0)
+        empty_y(1, 0)
+        first_layer(2)
+        first_layer(3)
+        second_layer(2)
+        empty_y(0, 1)
+        empty_y(2, 0)
+        second_layer(3)
+        empty_y(1, 1)
+        empty_y(3, 0)
+        empty_y(2, 1)
+        empty_y(3, 1)
+        for h in range(HALVES):
+            for e in range(E):
+                scatter(e, h)
+            nc.sync.dma_start(out[h * P : (h + 1) * P, :], placed[h][:])

@@ -1,7 +1,6 @@
 from contextlib import ExitStack
 
 import concourse.mybir as mybir
-from concourse.masks import make_identity
 
 K, T, E, C, H, N = 1024, 1280, 4, 256, 512, 256
 FLOPS = 2 * E * C * (K * H + H * N)
@@ -31,110 +30,137 @@ def tile_moe_two_mlp_gelu_kernel(
     with ExitStack() as ctx:
         keep = ctx.enter_context(tc.tile_pool(name="keep", bufs=1))
         work = ctx.enter_context(tc.tile_pool(name="work", bufs=2))
+        late = ctx.enter_context(tc.tile_pool(name="late", bufs=1))
         reuse = ctx.enter_context(tc.tile_pool(name="reuse", bufs=1))
         psum_a = ctx.enter_context(tc.psum_pool(name="psum_a", bufs=3))
         psum_t = ctx.enter_context(tc.psum_pool(name="psum_t", bufs=2))
         psum_y = ctx.enter_context(tc.psum_pool(name="psum_y", bufs=3))
 
+        W1_BYTES = PASSES * 2 * H
+        W2_BYTES = E * 2 * N
+        GATE_BYTES = 4 * SLOTS
+        ZCOLS = 16
+        at_gate = [GATE_BYTES, 0]
+        at_w1_first = at_gate[0] + GATE_BYTES - W1_BYTES
+        at_xw = at_w1_first + W1_BYTES
+        at_w1_rest = at_xw + 4 * PASSES * T
+        at_w2 = at_w1_rest + (E - 1) * W1_BYTES
+
         offs_sb = keep.tile([P, SLOTS // 16], U16, name="offs_sb")
         dst_sb = keep.tile([P, SLOTS // 16], U16, name="dst_sb")
-        xs = keep.tile([P, PASSES, T], U8, name="xs", align_bytes=64)
-        xw = [keep.tile([P, T], I32, name="xw%d" % o, align_bytes=64) for o in range(PASSES)]
+        xs = late.tile([P, PASSES, T], U8, name="xs", align_bytes=64, offset=at_gate[1])
+        blank = late.tile([P, P], F32, name="blank", align_bytes=64, offset=at_xw - 64)
         w1s = keep.tile([P, E * PASSES, H], U8, name="w1s", align_bytes=64)
         w2s = keep.tile([P, E, N], U8, name="w2s", align_bytes=64)
-        w1w = [keep.tile([P, PASSES, 2 * H], U8, name="w1w%d" % e, align_bytes=64) for e in range(E)]
-        w2w = keep.tile([P, E, 2 * N], U8, name="w2w", align_bytes=64)
-        gate_sb = keep.tile([P, HALVES, SLOTS], F32, name="gate_sb")
         placed = [keep.tile([P, T], F32, name="placed%d" % h) for h in range(HALVES)]
         ident = keep.tile([P, P], F32, name="ident")
-        zero = keep.tile([P, 1], F32, name="zero")
         warm = keep.tile([P, 1], F32, name="warm")
+        zero = late.tile([P, ZCOLS], F32, name="zero", offset=at_w2 - 32)
 
-        nc.vector.memset(xs[:].rearrange("p o t -> p (o t)").bitcast(I32), 0)
+        nc.gpsimd.memset(xs[:].rearrange("p o t -> p (o t)").bitcast(I32), 0)
+        nc.gpsimd.memset(blank[:], 0.0)
+        nc.gpsimd.affine_select(
+            out=ident[:],
+            in_=blank[:],
+            compare_op=mybir.AluOpType.not_equal,
+            fill=1.0,
+            base=0,
+            pattern=[[-1, P]],
+            channel_multiplier=1,
+        )
+        nc.vector.memset(zero[:], 0.0)
+        nc.vector.memset(placed[0][:], 0.0)
         nc.vector.memset(w1s[:].rearrange("p g i -> p (g i)").bitcast(I32), 0)
         nc.vector.memset(w2s[:].rearrange("p e n -> p (e n)").bitcast(I32), 0)
-        nc.gpsimd.memset(zero[:], 0.0)
-        make_identity(nc, ident[:])
-        nc.scalar.activation(warm[:], zero[:], GELU)
-        for h in range(HALVES):
-            nc.scalar.copy(placed[h][:], zero[:].to_broadcast([P, T]))
-
-        def load_w1(e):
-            nc.sync.dma_start(w1w[e][:].bitcast(I32), w1_words[e].rearrange("s p b -> p s b").bitcast(I32))
 
         nc.sync.dma_start(offs_sb[:], offs)
+        nc.sync.dma_start(dst_sb[:], dst)
         for q in range(4):
             nc.sync.dma_start(
                 xs[32 * q : 32 * q + 4].bitcast(I32),
                 x_scales[:, 4 * q : 4 * q + 4, :].rearrange("o f t -> f o t").bitcast(I32),
             )
+        xw = late.tile([P, PASSES, T], I32, name="xw", align_bytes=64, offset=at_xw)
         for o in range(PASSES):
-            nc.sync.dma_start(xw[o][:], x_words[o].rearrange("p t r -> p (t r)").bitcast(I32))
+            nc.sync.dma_start(xw[:, o, :], x_words[o].rearrange("p t r -> p (t r)").bitcast(I32))
+        w1_first = late.tile([P, PASSES, 2 * H], U8, name="w1_first", align_bytes=64, offset=at_w1_first)
+        nc.sync.dma_start(w1_first[:].bitcast(I32), w1_words[0].rearrange("s p b -> p s b").bitcast(I32))
         for q in range(4):
             nc.sync.dma_start(
                 w1s[32 * q : 32 * q + 4].bitcast(I32),
                 w1_scales[:, :, 4 * q : 4 * q + 4, :].rearrange("e s f i -> f (e s) i").bitcast(I32),
             )
-        load_w1(0)
-        load_w1(1)
         for q in range(4):
             nc.sync.dma_start(
                 w2s[32 * q : 32 * q + 4].bitcast(I32),
                 w2_scales[:, 0, 4 * q : 4 * q + 4, :].rearrange("e f n -> f e n").bitcast(I32),
             )
+
+        nc.scalar.activation(warm[:], zero[:, 0:1], GELU)
+        nc.scalar.copy(
+            placed[1][:].rearrange("p (r c) -> p r c", c=ZCOLS),
+            zero[:].unsqueeze(1).to_broadcast([P, T // ZCOLS, ZCOLS]),
+        )
+        w1_rest = late.tile([P, (E - 1) * PASSES, 2 * H], U8, name="w1_rest", align_bytes=64, offset=at_w1_rest)
+        nc.sync.dma_start(w1_rest[:].bitcast(I32), w1_words[1:].rearrange("e s p b -> p (e s) b").bitcast(I32))
+        w2w = late.tile([P, E, 2 * N], U8, name="w2w", align_bytes=64, offset=at_w2)
         nc.sync.dma_start(w2w[:].bitcast(I32), w2_words[:, 0].rearrange("e p b -> p e b").bitcast(I32))
-        load_w1(2)
-        load_w1(3)
-        nc.sync.dma_start(dst_sb[:], dst)
-        for h in range(HALVES):
-            nc.sync.dma_start(gate_sb[:, h, :], gate[h * P : (h + 1) * P, :])
+        gate_sb = {}
+
+        def load_gate(h):
+            gate_sb[h] = late.tile([P, SLOTS], F32, name="gate%d" % h, align_bytes=64, offset=at_gate[h])
+            nc.sync.dma_start(gate_sb[h][:], gate[h * P : (h + 1) * P, :])
 
         gw = {}
         gs = {}
         h_cols = {}
         y = {}
-        ysb = {}
-        H_BYTES = 2 * 4 * C
-        W_BYTES = 4 * C
-        over_words = {(2, 0): 0, (3, 0): H_BYTES}
-        over_y = {(0, 0): H_BYTES + W_BYTES, (0, 1): 2 * H_BYTES, (1, 1): 3 * H_BYTES}
+        ready = {}
+        KB = 1024
+        at_words = {(0, 0): 0, (0, 1): KB, (1, 0): 2 * KB, (1, 1): 3 * KB}
+        at_words.update({(2, 0): KB, (2, 1): 2 * KB, (3, 0): 4 * KB, (3, 1): 5 * KB})
+        at_scales = {(0, 0): 13 * KB, (0, 1): 14 * KB, (1, 0): 18 * KB, (1, 1): 0}
+        at_h = {0: 4 * KB, 1: 10 * KB, 2: 6 * KB, 3: 8 * KB}
+        at_y = {(0, 0): 10 * KB, (0, 1): 6 * KB, (2, 0): 8 * KB, (3, 0): 12 * KB, (1, 1): 12 * KB}
+        at_y.update({(1, 0): 15 * KB, (2, 1): 16 * KB, (3, 1): 17 * KB})
 
         def gather_scales(pair):
             cols = offs_sb[:, 2 * pair * LIST_COLS : 2 * (pair + 1) * LIST_COLS]
             for o in range(PASSES):
-                gs[pair, o] = keep.tile([P, 2 * C], U8, name="gs%d_%d" % (pair, o), align_bytes=64)
+                name = "gs%d_%d" % (pair, o)
+                gs[pair, o] = reuse.tile([P, 2 * C], U8, name=name, align_bytes=64, offset=at_scales[pair, o])
                 nc.vector.tensor_copy(gs[pair, o][:], xs[:, o, :].indirect(cols))
 
-        def gather_words(e, o):
+        def gather_words(e):
             cols = offs_sb[:, e * LIST_COLS : (e + 1) * LIST_COLS]
-            name = "gw%d_%d" % (e, o)
-            if (e, o) in over_words:
-                gw[e, o] = reuse.tile([P, C], U32, name=name, align_bytes=64, offset=over_words[e, o])
-            else:
-                gw[e, o] = keep.tile([P, C], U32, name=name, align_bytes=64)
-            nc.vector.tensor_copy(gw[e, o][:], xw[o][:].bitcast(U32).indirect(cols))
+            for o in range(PASSES):
+                name = "gw%d_%d" % (e, o)
+                gw[e, o] = reuse.tile([P, C], U32, name=name, align_bytes=64, offset=at_words[e, o])
+                nc.vector.tensor_copy(gw[e, o][:], xw[:, o, :].bitcast(U32).indirect(cols))
 
         def first_layer(e):
             turned = psum_t.tile([P, 2, C], F32, name="turned")
-            for c in range(C // P):
-                acc = psum_a.tile([P, H], F32, name="acc")
-                s0 = (e % 2) * C + c * P
-                for o in range(PASSES):
+            acc = [psum_a.tile([P, H], F32, name="acc") for c in range(C // P)]
+            for o in range(PASSES):
+                w1_pass = w1_first[:, o, :] if e == 0 else w1_rest[:, (e - 1) * PASSES + o, :]
+                for c in range(C // P):
+                    s0 = (e % 2) * C + c * P
                     nc.tensor.matmul_mx(
-                        out=acc[:],
+                        out=acc[c][:],
                         lhsT=gw[e, o][:, c * P : (c + 1) * P].bitcast(FP8X4),
                         lhsT_scale=gs[e // 2, o][:, s0 : s0 + P],
-                        rhs=w1w[e][:, o, :].bitcast(FP4X4),
+                        rhs=w1_pass.bitcast(FP4X4),
                         rhs_scale=w1s[:, e * PASSES + o, :],
                         start=(o == 0),
                         stop=(o == PASSES - 1),
                     )
+            for c in range(C // P):
                 h_rows = work.tile([P, 2, P, 2], BF16, name="h_rows", bufs=4)
-                nc.scalar.activation(h_rows[:], acc[:].rearrange("s (p u d) -> s u p d", u=2, d=2), GELU)
+                nc.scalar.activation(h_rows[:], acc[c][:].rearrange("s (p u d) -> s u p d", u=2, d=2), GELU)
                 h_pairs = h_rows[:].rearrange("s u p d -> s (u p d)").bitcast(F32)
                 for u in range(2):
                     nc.tensor.transpose(turned[:, u, c * P : (c + 1) * P], h_pairs[:, u * P : (u + 1) * P], ident[:])
-            h_cols[e] = reuse.tile([P, 4 * C], BF16, name="h_cols%d" % e, align_bytes=64, offset=e * H_BYTES)
+            h_cols[e] = reuse.tile([P, 4 * C], BF16, name="h_cols%d" % e, align_bytes=64, offset=at_h[e])
             nc.scalar.copy(
                 h_cols[e][:].bitcast(F32).rearrange("p (s u) -> p s u", u=2), turned[:].rearrange("p u s -> p s u")
             )
@@ -156,45 +182,43 @@ def tile_moe_two_mlp_gelu_kernel(
                 )
 
         def empty_y(e, h):
-            name = "ysb%d_%d" % (e, h)
-            if (e, h) in over_y:
-                ysb[e, h] = reuse.tile([P, C], F32, name=name, align_bytes=64, offset=over_y[e, h])
-            else:
-                ysb[e, h] = keep.tile([P, C], F32, name=name, align_bytes=64)
-            nc.scalar.copy(ysb[e, h][:], y[e][:, h, :])
+            ready[e, h] = reuse.tile([P, C], F32, name="ready%d_%d" % (e, h), align_bytes=64, offset=at_y[e, h])
+            nc.vector.tensor_tensor(ready[e, h][:], y[e][:, h, :], gate_sb[h][:, e * C : (e + 1) * C], MULT)
 
         def scatter(e, h):
             cols = dst_sb[:, e * LIST_COLS : (e + 1) * LIST_COLS]
-            nc.vector.tensor_tensor(
-                placed[h][:].indirect(cols), ysb[e, h][:], gate_sb[:, h, e * C : (e + 1) * C], MULT
-            )
+            nc.vector.tensor_copy(placed[h][:].indirect(cols), ready[e, h][:])
 
         gather_scales(0)
-        for e in range(2):
-            for o in range(PASSES):
-                gather_words(e, o)
-        gather_scales(1)
-        gather_words(2, 1)
-        gather_words(3, 1)
+        gather_words(0)
+        gather_words(1)
         first_layer(0)
+        load_gate(0)
         first_layer(1)
+        gather_scales(1)
+        load_gate(1)
+        gather_words(2)
         second_layer(0)
-        gather_words(2, 0)
+        gather_words(3)
         second_layer(1)
-        gather_words(3, 0)
         empty_y(0, 0)
         empty_y(1, 0)
         first_layer(2)
         first_layer(3)
+        scatter(0, 0)
+        scatter(1, 0)
         second_layer(2)
         empty_y(0, 1)
-        empty_y(2, 0)
+        scatter(0, 1)
         second_layer(3)
-        empty_y(1, 1)
-        empty_y(3, 0)
+        empty_y(2, 0)
         empty_y(2, 1)
+        scatter(2, 0)
+        empty_y(3, 0)
         empty_y(3, 1)
-        for h in range(HALVES):
-            for e in range(E):
-                scatter(e, h)
-            nc.sync.dma_start(out[h * P : (h + 1) * P, :], placed[h][:])
+        scatter(3, 0)
+        nc.sync.dma_start(out[0:P, :], placed[0][:])
+        empty_y(1, 1)
+        for e in (1, 2, 3):
+            scatter(e, 1)
+        nc.sync.dma_start(out[P : 2 * P, :], placed[1][:])

@@ -1,6 +1,7 @@
 from contextlib import ExitStack
 
 import concourse.mybir as mybir
+from concourse.masks import make_identity
 
 K, T, E, C, H, N = 1024, 1280, 4, 256, 512, 256
 FLOPS = 2 * E * C * (K * H + H * N)
@@ -30,137 +31,147 @@ def tile_moe_two_mlp_gelu_kernel(
     with ExitStack() as ctx:
         keep = ctx.enter_context(tc.tile_pool(name="keep", bufs=1))
         work = ctx.enter_context(tc.tile_pool(name="work", bufs=2))
-        late = ctx.enter_context(tc.tile_pool(name="late", bufs=1))
         reuse = ctx.enter_context(tc.tile_pool(name="reuse", bufs=1))
-        psum_a = ctx.enter_context(tc.psum_pool(name="psum_a", bufs=3))
-        psum_t = ctx.enter_context(tc.psum_pool(name="psum_t", bufs=2))
+        psum_a = ctx.enter_context(tc.psum_pool(name="psum_a", bufs=4))
+        psum_t = ctx.enter_context(tc.psum_pool(name="psum_t", bufs=1))
         psum_y = ctx.enter_context(tc.psum_pool(name="psum_y", bufs=3))
 
-        W1_BYTES = PASSES * 2 * H
-        W2_BYTES = E * 2 * N
-        GATE_BYTES = 4 * SLOTS
         ZCOLS = 16
-        at_gate = [GATE_BYTES, 0]
-        at_w1_first = at_gate[0] + GATE_BYTES - W1_BYTES
-        at_xw = at_w1_first + W1_BYTES
-        at_w1_rest = at_xw + 4 * PASSES * T
-        at_w2 = at_w1_rest + (E - 1) * W1_BYTES
-
         offs_sb = keep.tile([P, SLOTS // 16], U16, name="offs_sb")
         dst_sb = keep.tile([P, SLOTS // 16], U16, name="dst_sb")
-        xs = late.tile([P, PASSES, T], U8, name="xs", align_bytes=64, offset=at_gate[1])
-        blank = late.tile([P, P], F32, name="blank", align_bytes=64, offset=at_xw - 64)
+        xs = keep.tile([P, PASSES, T], U8, name="xs", align_bytes=64)
+        xw = [keep.tile([P, T], I32, name="xw%d" % o, align_bytes=64) for o in range(PASSES)]
         w1s = keep.tile([P, E * PASSES, H], U8, name="w1s", align_bytes=64)
         w2s = keep.tile([P, E, N], U8, name="w2s", align_bytes=64)
+        w1w = {}
+        w2w = keep.tile([P, E, 2 * N], U8, name="w2w", align_bytes=64)
+        gate_sb = [keep.tile([P, SLOTS], F32, name="gate%d" % h) for h in range(HALVES)]
         placed = [keep.tile([P, T], F32, name="placed%d" % h) for h in range(HALVES)]
         ident = keep.tile([P, P], F32, name="ident")
         warm = keep.tile([P, 1], F32, name="warm")
-        zero = late.tile([P, ZCOLS], F32, name="zero", offset=at_w2 - 32)
+        zero = keep.tile([P, ZCOLS], F32, name="zero")
 
         nc.gpsimd.memset(xs[:].rearrange("p o t -> p (o t)").bitcast(I32), 0)
-        nc.gpsimd.memset(blank[:], 0.0)
-        nc.gpsimd.affine_select(
-            out=ident[:],
-            in_=blank[:],
-            compare_op=mybir.AluOpType.not_equal,
-            fill=1.0,
-            base=0,
-            pattern=[[-1, P]],
-            channel_multiplier=1,
-        )
-        nc.vector.memset(zero[:], 0.0)
-        nc.vector.memset(placed[0][:], 0.0)
+        nc.gpsimd.memset(zero[:], 0.0)
         nc.vector.memset(w1s[:].rearrange("p g i -> p (g i)").bitcast(I32), 0)
         nc.vector.memset(w2s[:].rearrange("p e n -> p (e n)").bitcast(I32), 0)
+        make_identity(nc, ident[:])
+
+        def load_w1(first, end):
+            tile = keep.tile([P, (end - first) * PASSES, 2 * H], U8, name="w1w%d" % first, align_bytes=64)
+            nc.sync.dma_start(tile[:].bitcast(I32), w1_words[first:end].rearrange("e s p b -> p (e s) b").bitcast(I32))
+            for e in range(first, end):
+                for o in range(PASSES):
+                    w1w[e, o] = tile[:, (e - first) * PASSES + o, :]
+
+        def load_words(o):
+            nc.sync.dma_start(xw[o][:], x_words[o].rearrange("p t r -> p (t r)").bitcast(I32))
 
         nc.sync.dma_start(offs_sb[:], offs)
         nc.sync.dma_start(dst_sb[:], dst)
         for q in range(4):
-            nc.sync.dma_start(
+            queue = nc.scalar if q < 2 else nc.sync
+            queue.dma_start(
                 xs[32 * q : 32 * q + 4].bitcast(I32),
                 x_scales[:, 4 * q : 4 * q + 4, :].rearrange("o f t -> f o t").bitcast(I32),
             )
-        xw = late.tile([P, PASSES, T], I32, name="xw", align_bytes=64, offset=at_xw)
-        for o in range(PASSES):
-            nc.sync.dma_start(xw[:, o, :], x_words[o].rearrange("p t r -> p (t r)").bitcast(I32))
-        w1_first = late.tile([P, PASSES, 2 * H], U8, name="w1_first", align_bytes=64, offset=at_w1_first)
-        nc.sync.dma_start(w1_first[:].bitcast(I32), w1_words[0].rearrange("s p b -> p s b").bitcast(I32))
+        load_words(0)
+        load_w1(0, 1)
         for q in range(4):
-            nc.sync.dma_start(
+            nc.scalar.dma_start(
                 w1s[32 * q : 32 * q + 4].bitcast(I32),
                 w1_scales[:, :, 4 * q : 4 * q + 4, :].rearrange("e s f i -> f (e s) i").bitcast(I32),
             )
+        load_words(1)
+        load_w1(1, 2)
+        nc.sync.dma_start(w2w[:].bitcast(I32), w2_words[:, 0].rearrange("e p b -> p e b").bitcast(I32))
+        for h in range(HALVES):
+            nc.sync.dma_start(gate_sb[h][:], gate[h * P : (h + 1) * P, :])
+        load_w1(2, 4)
+
+        nc.scalar.activation(warm[:], zero[:, 0:1], GELU)
+        for h in range(HALVES):
+            nc.scalar.copy(
+                placed[h][:].rearrange("p (r c) -> p r c", c=ZCOLS),
+                zero[:].unsqueeze(1).to_broadcast([P, T // ZCOLS, ZCOLS]),
+            )
         for q in range(4):
-            nc.sync.dma_start(
+            nc.scalar.dma_start(
                 w2s[32 * q : 32 * q + 4].bitcast(I32),
                 w2_scales[:, 0, 4 * q : 4 * q + 4, :].rearrange("e f n -> f e n").bitcast(I32),
             )
-
-        nc.scalar.activation(warm[:], zero[:, 0:1], GELU)
-        nc.scalar.copy(
-            placed[1][:].rearrange("p (r c) -> p r c", c=ZCOLS),
-            zero[:].unsqueeze(1).to_broadcast([P, T // ZCOLS, ZCOLS]),
-        )
-        w1_rest = late.tile([P, (E - 1) * PASSES, 2 * H], U8, name="w1_rest", align_bytes=64, offset=at_w1_rest)
-        nc.sync.dma_start(w1_rest[:].bitcast(I32), w1_words[1:].rearrange("e s p b -> p (e s) b").bitcast(I32))
-        w2w = late.tile([P, E, 2 * N], U8, name="w2w", align_bytes=64, offset=at_w2)
-        nc.sync.dma_start(w2w[:].bitcast(I32), w2_words[:, 0].rearrange("e p b -> p e b").bitcast(I32))
-        gate_sb = {}
-
-        def load_gate(h):
-            gate_sb[h] = late.tile([P, SLOTS], F32, name="gate%d" % h, align_bytes=64, offset=at_gate[h])
-            nc.sync.dma_start(gate_sb[h][:], gate[h * P : (h + 1) * P, :])
 
         gw = {}
         gs = {}
         h_cols = {}
         y = {}
         ready = {}
-        KB = 1024
-        at_words = {(0, 0): 0, (0, 1): KB, (1, 0): 2 * KB, (1, 1): 3 * KB}
-        at_words.update({(2, 0): KB, (2, 1): 2 * KB, (3, 0): 4 * KB, (3, 1): 5 * KB})
-        at_scales = {(0, 0): 13 * KB, (0, 1): 14 * KB, (1, 0): 18 * KB, (1, 1): 0}
-        at_h = {0: 4 * KB, 1: 10 * KB, 2: 6 * KB, 3: 8 * KB}
-        at_y = {(0, 0): 10 * KB, (0, 1): 6 * KB, (2, 0): 8 * KB, (3, 0): 12 * KB, (1, 1): 12 * KB}
-        at_y.update({(1, 0): 15 * KB, (2, 1): 16 * KB, (3, 1): 17 * KB})
+        H_BYTES = 2 * 4 * C
+        W_BYTES = 4 * C
+        follows_rows = {(1, 1): (2, 1), (2, 1): (3, 1)}
+        at_words = {(0, 0): 0, (0, 1): 1, (2, 0): 0, (3, 0): 1}
+        at_rows = {key: H_BYTES + (2 + i) * W_BYTES for i, key in enumerate([(0, 0), (2, 1), (3, 1)])}
 
-        def gather_scales(pair):
+        def gather_scales(pair, o):
             cols = offs_sb[:, 2 * pair * LIST_COLS : 2 * (pair + 1) * LIST_COLS]
-            for o in range(PASSES):
-                name = "gs%d_%d" % (pair, o)
-                gs[pair, o] = reuse.tile([P, 2 * C], U8, name=name, align_bytes=64, offset=at_scales[pair, o])
-                nc.vector.tensor_copy(gs[pair, o][:], xs[:, o, :].indirect(cols))
+            name = "gs%d_%d" % (pair, o)
+            if (pair, o) == (1, 1):
+                gs[pair, o] = reuse.tile([P, 2 * C], U8, name=name, align_bytes=64, offset=0)
+            elif (pair, o) == (1, 0):
+                gs[pair, o] = reuse.tile([P, 2 * C], U8, name=name, align_bytes=64, offset=at_rows[0, 0])
+            else:
+                gs[pair, o] = keep.tile([P, 2 * C], U8, name=name, align_bytes=64)
+            nc.vector.tensor_copy(gs[pair, o][:], xs[:, o, :].indirect(cols))
 
-        def gather_words(e):
+        def gather_words(e, o):
             cols = offs_sb[:, e * LIST_COLS : (e + 1) * LIST_COLS]
-            for o in range(PASSES):
-                name = "gw%d_%d" % (e, o)
-                gw[e, o] = reuse.tile([P, C], U32, name=name, align_bytes=64, offset=at_words[e, o])
-                nc.vector.tensor_copy(gw[e, o][:], xw[:, o, :].bitcast(U32).indirect(cols))
+            name = "gw%d_%d" % (e, o)
+            if (e, o) in at_words:
+                at = H_BYTES + at_words[e, o] * W_BYTES
+                gw[e, o] = reuse.tile([P, C], U32, name=name, align_bytes=64, offset=at)
+            else:
+                gw[e, o] = keep.tile([P, C], U32, name=name, align_bytes=64)
+            nc.vector.tensor_copy(gw[e, o][:], xw[o][:].bitcast(U32).indirect(cols))
 
-        def first_layer(e):
-            turned = psum_t.tile([P, 2, C], F32, name="turned")
-            acc = [psum_a.tile([P, H], F32, name="acc") for c in range(C // P)]
+        acc = {}
+        h_rows = {}
+
+        def first_pass(e, c, o):
+            if o == 0:
+                acc[e, c] = psum_a.tile([P, H], F32, name="acc")
+            s0 = (e % 2) * C + c * P
+            nc.tensor.matmul_mx(
+                out=acc[e, c][:],
+                lhsT=gw[e, o][:, c * P : (c + 1) * P].bitcast(FP8X4),
+                lhsT_scale=gs[e // 2, o][:, s0 : s0 + P],
+                rhs=w1w[e, o].bitcast(FP4X4),
+                rhs_scale=w1s[:, e * PASSES + o, :],
+                start=(o == 0),
+                stop=(o == PASSES - 1),
+            )
+            if o == PASSES - 1:
+                if (e, c) in at_rows:
+                    name = "h_rows%d_%d" % (e, c)
+                    rows = reuse.tile([P, 2, P, 2], BF16, name=name, align_bytes=64, offset=at_rows[e, c])
+                else:
+                    rows = work.tile([P, 2, P, 2], BF16, name="h_rows", bufs=4)
+                nc.scalar.activation(rows[:], acc[e, c][:].rearrange("s (p u d) -> s u p d", u=2, d=2), GELU)
+                h_rows[e, c] = rows
+
+        def first_product(e, c):
             for o in range(PASSES):
-                w1_pass = w1_first[:, o, :] if e == 0 else w1_rest[:, (e - 1) * PASSES + o, :]
-                for c in range(C // P):
-                    s0 = (e % 2) * C + c * P
-                    nc.tensor.matmul_mx(
-                        out=acc[c][:],
-                        lhsT=gw[e, o][:, c * P : (c + 1) * P].bitcast(FP8X4),
-                        lhsT_scale=gs[e // 2, o][:, s0 : s0 + P],
-                        rhs=w1_pass.bitcast(FP4X4),
-                        rhs_scale=w1s[:, e * PASSES + o, :],
-                        start=(o == 0),
-                        stop=(o == PASSES - 1),
-                    )
+                first_pass(e, c, o)
+
+        def turn(e):
+            turned = psum_t.tile([P, 2, C], F32, name="turned")
             for c in range(C // P):
-                h_rows = work.tile([P, 2, P, 2], BF16, name="h_rows", bufs=4)
-                nc.scalar.activation(h_rows[:], acc[c][:].rearrange("s (p u d) -> s u p d", u=2, d=2), GELU)
-                h_pairs = h_rows[:].rearrange("s u p d -> s (u p d)").bitcast(F32)
+                h_pairs = h_rows[e, c][:].rearrange("s u p d -> s (u p d)").bitcast(F32)
                 for u in range(2):
                     nc.tensor.transpose(turned[:, u, c * P : (c + 1) * P], h_pairs[:, u * P : (u + 1) * P], ident[:])
-            h_cols[e] = reuse.tile([P, 4 * C], BF16, name="h_cols%d" % e, align_bytes=64, offset=at_h[e])
+            if e == 0:
+                h_cols[e] = reuse.tile([P, 4 * C], BF16, name="h_cols_first", align_bytes=64, offset=0)
+            else:
+                h_cols[e] = keep.tile([P, 4 * C], BF16, name="h_cols%d" % e, align_bytes=64)
             nc.scalar.copy(
                 h_cols[e][:].bitcast(F32).rearrange("p (s u) -> p s u", u=2), turned[:].rearrange("p u s -> p s u")
             )
@@ -182,43 +193,57 @@ def tile_moe_two_mlp_gelu_kernel(
                 )
 
         def empty_y(e, h):
-            ready[e, h] = reuse.tile([P, C], F32, name="ready%d_%d" % (e, h), align_bytes=64, offset=at_y[e, h])
-            nc.vector.tensor_tensor(ready[e, h][:], y[e][:, h, :], gate_sb[h][:, e * C : (e + 1) * C], MULT)
+            name = "ready%d_%d" % (e, h)
+            if (e, h) in follows_rows:
+                ready[e, h] = reuse.tile([P, C], F32, name=name, align_bytes=64, offset=at_rows[follows_rows[e, h]])
+            else:
+                ready[e, h] = keep.tile([P, C], F32, name=name, align_bytes=64)
+            nc.scalar.copy(ready[e, h][:], y[e][:, h, :])
 
         def scatter(e, h):
             cols = dst_sb[:, e * LIST_COLS : (e + 1) * LIST_COLS]
-            nc.vector.tensor_copy(placed[h][:].indirect(cols), ready[e, h][:])
+            nc.vector.tensor_tensor(
+                placed[h][:].indirect(cols), ready[e, h][:], gate_sb[h][:, e * C : (e + 1) * C], MULT
+            )
 
-        gather_scales(0)
-        gather_words(0)
-        gather_words(1)
-        first_layer(0)
-        load_gate(0)
-        first_layer(1)
-        gather_scales(1)
-        load_gate(1)
-        gather_words(2)
+        gather_scales(0, 0)
+        gather_scales(0, 1)
+        for e in (0, 1):
+            for o in range(PASSES):
+                gather_words(e, o)
+        gather_words(2, 1)
+        gather_words(3, 1)
+        for o in range(PASSES):
+            for c in range(C // P):
+                first_pass(0, c, o)
+        gather_words(2, 0)
+        gather_words(3, 0)
+        first_product(1, 0)
+        turn(0)
+        gather_scales(1, 0)
+        first_product(1, 1)
+        turn(1)
         second_layer(0)
-        gather_words(3)
-        second_layer(1)
+        gather_scales(1, 1)
         empty_y(0, 0)
-        empty_y(1, 0)
-        first_layer(2)
-        first_layer(3)
-        scatter(0, 0)
-        scatter(1, 0)
-        second_layer(2)
         empty_y(0, 1)
-        scatter(0, 1)
-        second_layer(3)
+        first_product(2, 0)
+        second_layer(1)
+        empty_y(1, 0)
+        first_product(2, 1)
+        first_product(3, 0)
+        first_product(3, 1)
+        turn(2)
+        empty_y(1, 1)
+        second_layer(2)
+        turn(3)
         empty_y(2, 0)
         empty_y(2, 1)
-        scatter(2, 0)
+        second_layer(3)
         empty_y(3, 0)
         empty_y(3, 1)
-        scatter(3, 0)
-        nc.sync.dma_start(out[0:P, :], placed[0][:])
-        empty_y(1, 1)
-        for e in (1, 2, 3):
-            scatter(e, 1)
-        nc.sync.dma_start(out[P : 2 * P, :], placed[1][:])
+        for e in range(E):
+            for h in range(HALVES):
+                scatter(e, h)
+        for h in range(HALVES):
+            nc.sync.dma_start(out[h * P : (h + 1) * P, :], placed[h][:])

@@ -40,7 +40,7 @@ def tile_moe_two_mlp_gelu_kernel(
         offs_sb = keep.tile([P, SLOTS // 16], U16, name="offs_sb")
         dst_sb = keep.tile([P, SLOTS // 16], U16, name="dst_sb")
         xs = keep.tile([P, PASSES, T], U8, name="xs", align_bytes=64)
-        xw = [keep.tile([P, T], I32, name="xw%d" % o, align_bytes=64) for o in range(PASSES)]
+        xw = keep.tile([P, PASSES, T], I32, name="xw", align_bytes=64)
         w1s = keep.tile([P, E * PASSES, H], U8, name="w1s", align_bytes=64)
         w2s = keep.tile([P, E, N], U8, name="w2s", align_bytes=64)
         w1w = {}
@@ -52,7 +52,7 @@ def tile_moe_two_mlp_gelu_kernel(
         zero = keep.tile([P, ZCOLS], F32, name="zero")
 
         nc.gpsimd.memset(xs[:].rearrange("p o t -> p (o t)").bitcast(I32), 0)
-        nc.gpsimd.memset(zero[:], 0.0)
+        nc.vector.memset(zero[:], 0.0)
         nc.vector.memset(w1s[:].rearrange("p g i -> p (g i)").bitcast(I32), 0)
         nc.vector.memset(w2s[:].rearrange("p e n -> p (e n)").bitcast(I32), 0)
         make_identity(nc, ident[:])
@@ -64,27 +64,27 @@ def tile_moe_two_mlp_gelu_kernel(
                 for o in range(PASSES):
                     w1w[e, o] = tile[:, (e - first) * PASSES + o, :]
 
-        def load_words(o):
-            nc.sync.dma_start(xw[o][:], x_words[o].rearrange("p t r -> p (t r)").bitcast(I32))
-
         nc.sync.dma_start(offs_sb[:], offs)
         nc.sync.dma_start(dst_sb[:], dst)
         for q in range(4):
-            queue = nc.scalar if q < 2 else nc.sync
-            queue.dma_start(
+            nc.sync.dma_start(
                 xs[32 * q : 32 * q + 4].bitcast(I32),
                 x_scales[:, 4 * q : 4 * q + 4, :].rearrange("o f t -> f o t").bitcast(I32),
             )
-        load_words(0)
+        nc.sync.dma_start(xw[:], x_words.rearrange("o p t r -> p o (t r)").bitcast(I32))
         load_w1(0, 1)
         for q in range(4):
-            nc.scalar.dma_start(
+            nc.sync.dma_start(
                 w1s[32 * q : 32 * q + 4].bitcast(I32),
                 w1_scales[:, :, 4 * q : 4 * q + 4, :].rearrange("e s f i -> f (e s) i").bitcast(I32),
             )
-        load_words(1)
         load_w1(1, 2)
         nc.sync.dma_start(w2w[:].bitcast(I32), w2_words[:, 0].rearrange("e p b -> p e b").bitcast(I32))
+        for q in range(4):
+            nc.sync.dma_start(
+                w2s[32 * q : 32 * q + 4].bitcast(I32),
+                w2_scales[:, 0, 4 * q : 4 * q + 4, :].rearrange("e f n -> f e n").bitcast(I32),
+            )
         for h in range(HALVES):
             nc.sync.dma_start(gate_sb[h][:], gate[h * P : (h + 1) * P, :])
         load_w1(2, 4)
@@ -95,11 +95,6 @@ def tile_moe_two_mlp_gelu_kernel(
                 placed[h][:].rearrange("p (r c) -> p r c", c=ZCOLS),
                 zero[:].unsqueeze(1).to_broadcast([P, T // ZCOLS, ZCOLS]),
             )
-        for q in range(4):
-            nc.scalar.dma_start(
-                w2s[32 * q : 32 * q + 4].bitcast(I32),
-                w2_scales[:, 0, 4 * q : 4 * q + 4, :].rearrange("e f n -> f e n").bitcast(I32),
-            )
 
         gw = {}
         gs = {}
@@ -109,8 +104,7 @@ def tile_moe_two_mlp_gelu_kernel(
         H_BYTES = 2 * 4 * C
         W_BYTES = 4 * C
         follows_rows = {(1, 1): (2, 1), (2, 1): (3, 1)}
-        at_words = {(0, 0): 0, (0, 1): 1, (2, 0): 0, (3, 0): 1}
-        at_rows = {key: H_BYTES + (2 + i) * W_BYTES for i, key in enumerate([(0, 0), (2, 1), (3, 1)])}
+        at_rows = {key: H_BYTES + i * W_BYTES for i, key in enumerate([(0, 0), (2, 1), (3, 1)])}
 
         def gather_scales(pair, o):
             cols = offs_sb[:, 2 * pair * LIST_COLS : 2 * (pair + 1) * LIST_COLS]
@@ -125,13 +119,8 @@ def tile_moe_two_mlp_gelu_kernel(
 
         def gather_words(e, o):
             cols = offs_sb[:, e * LIST_COLS : (e + 1) * LIST_COLS]
-            name = "gw%d_%d" % (e, o)
-            if (e, o) in at_words:
-                at = H_BYTES + at_words[e, o] * W_BYTES
-                gw[e, o] = reuse.tile([P, C], U32, name=name, align_bytes=64, offset=at)
-            else:
-                gw[e, o] = keep.tile([P, C], U32, name=name, align_bytes=64)
-            nc.vector.tensor_copy(gw[e, o][:], xw[o][:].bitcast(U32).indirect(cols))
+            gw[e, o] = keep.tile([P, C], U32, name="gw%d_%d" % (e, o), align_bytes=64)
+            nc.vector.tensor_copy(gw[e, o][:], xw[:, o, :].bitcast(U32).indirect(cols))
 
         acc = {}
         h_rows = {}
@@ -208,16 +197,11 @@ def tile_moe_two_mlp_gelu_kernel(
 
         gather_scales(0, 0)
         gather_scales(0, 1)
-        for e in (0, 1):
+        for e in range(E):
             for o in range(PASSES):
                 gather_words(e, o)
-        gather_words(2, 1)
-        gather_words(3, 1)
-        for o in range(PASSES):
-            for c in range(C // P):
-                first_pass(0, c, o)
-        gather_words(2, 0)
-        gather_words(3, 0)
+        first_product(0, 0)
+        first_product(0, 1)
         first_product(1, 0)
         turn(0)
         gather_scales(1, 0)

@@ -41,7 +41,7 @@ def tile_moe_two_mlp_gelu_kernel(
         dst_sb = keep.tile([P, SLOTS // 16], U16, name="dst_sb")
         xs = keep.tile([P, PASSES, T], U8, name="xs", align_bytes=64)
         xw = keep.tile([P, PASSES, T], I32, name="xw", align_bytes=64)
-        w1s = keep.tile([P, E * PASSES, H], U8, name="w1s", align_bytes=64)
+        w1s = [keep.tile([P, 2 * PASSES, H], U8, name="w1s%d" % pair, align_bytes=64) for pair in range(2)]
         w2s = keep.tile([P, E, N], U8, name="w2s", align_bytes=64)
         w1w = {}
         w2w = keep.tile([P, E, 2 * N], U8, name="w2w", align_bytes=64)
@@ -53,8 +53,9 @@ def tile_moe_two_mlp_gelu_kernel(
 
         nc.gpsimd.memset(xs[:].rearrange("p o t -> p (o t)").bitcast(I32), 0)
         nc.vector.memset(zero[:], 0.0)
-        nc.vector.memset(w1s[:].rearrange("p g i -> p (g i)").bitcast(I32), 0)
-        nc.vector.memset(w2s[:].rearrange("p e n -> p (e n)").bitcast(I32), 0)
+        nc.gpsimd.memset(w1s[0][:].rearrange("p g i -> p (g i)").bitcast(I32), 0)
+        nc.gpsimd.memset(w2s[:].rearrange("p e n -> p (e n)").bitcast(I32), 0)
+        nc.gpsimd.memset(w1s[1][:].rearrange("p g i -> p (g i)").bitcast(I32), 0)
         make_identity(nc, ident[:])
 
         def load_w1(first, end):
@@ -63,6 +64,13 @@ def tile_moe_two_mlp_gelu_kernel(
             for e in range(first, end):
                 for o in range(PASSES):
                     w1w[e, o] = tile[:, (e - first) * PASSES + o, :]
+
+        def load_w1_scales(pair):
+            for q in range(4):
+                rows = w1_scales[2 * pair : 2 * pair + 2, :, 4 * q : 4 * q + 4, :]
+                nc.sync.dma_start(
+                    w1s[pair][32 * q : 32 * q + 4].bitcast(I32), rows.rearrange("e s f i -> f (e s) i").bitcast(I32)
+                )
 
         nc.sync.dma_start(offs_sb[:], offs)
         nc.sync.dma_start(dst_sb[:], dst)
@@ -73,11 +81,7 @@ def tile_moe_two_mlp_gelu_kernel(
             )
         nc.sync.dma_start(xw[:], x_words.rearrange("o p t r -> p o (t r)").bitcast(I32))
         load_w1(0, 1)
-        for q in range(4):
-            nc.sync.dma_start(
-                w1s[32 * q : 32 * q + 4].bitcast(I32),
-                w1_scales[:, :, 4 * q : 4 * q + 4, :].rearrange("e s f i -> f (e s) i").bitcast(I32),
-            )
+        load_w1_scales(0)
         load_w1(1, 2)
         nc.sync.dma_start(w2w[:].bitcast(I32), w2_words[:, 0].rearrange("e p b -> p e b").bitcast(I32))
         for q in range(4):
@@ -85,9 +89,10 @@ def tile_moe_two_mlp_gelu_kernel(
                 w2s[32 * q : 32 * q + 4].bitcast(I32),
                 w2_scales[:, 0, 4 * q : 4 * q + 4, :].rearrange("e f n -> f e n").bitcast(I32),
             )
-        for h in range(HALVES):
-            nc.sync.dma_start(gate_sb[h][:], gate[h * P : (h + 1) * P, :])
+        nc.sync.dma_start(gate_sb[0][:], gate[0:P, :])
+        load_w1_scales(1)
         load_w1(2, 4)
+        nc.sync.dma_start(gate_sb[1][:], gate[P : 2 * P, :])
 
         nc.scalar.activation(warm[:], zero[:, 0:1], GELU)
         for h in range(HALVES):
@@ -134,7 +139,7 @@ def tile_moe_two_mlp_gelu_kernel(
                 lhsT=gw[e, o][:, c * P : (c + 1) * P].bitcast(FP8X4),
                 lhsT_scale=gs[e // 2, o][:, s0 : s0 + P],
                 rhs=w1w[e, o].bitcast(FP4X4),
-                rhs_scale=w1s[:, e * PASSES + o, :],
+                rhs_scale=w1s[e // 2][:, (e % 2) * PASSES + o, :],
                 start=(o == 0),
                 stop=(o == PASSES - 1),
             )

@@ -22,6 +22,10 @@ PASSES = K // 512
 SLOTS = E * C
 LIST_COLS = C // 16
 HALVES = N // P
+SHIFT = 16
+ZCOLS = 16
+ZPIECE = 640
+KIB = 1024
 
 
 def tile_moe_two_mlp_gelu_kernel(
@@ -30,209 +34,249 @@ def tile_moe_two_mlp_gelu_kernel(
     nc = tc.nc
     with ExitStack() as ctx:
         keep = ctx.enter_context(tc.tile_pool(name="keep", bufs=1))
-        work = ctx.enter_context(tc.tile_pool(name="work", bufs=2))
         reuse = ctx.enter_context(tc.tile_pool(name="reuse", bufs=1))
-        psum_a = ctx.enter_context(tc.psum_pool(name="psum_a", bufs=4))
-        psum_t = ctx.enter_context(tc.psum_pool(name="psum_t", bufs=1))
-        psum_y = ctx.enter_context(tc.psum_pool(name="psum_y", bufs=3))
+        psum = ctx.enter_context(tc.psum_pool(name="psum", bufs=1))
 
-        ZCOLS = 16
         offs_sb = keep.tile([P, SLOTS // 16], U16, name="offs_sb")
         dst_sb = keep.tile([P, SLOTS // 16], U16, name="dst_sb")
-        xs = keep.tile([P, PASSES, T], U8, name="xs", align_bytes=64)
-        xw = keep.tile([P, PASSES, T], I32, name="xw", align_bytes=64)
+        xs = keep.tile([P, T], U8, name="xs", align_bytes=64)
+        xw = [keep.tile([P, T], I32, name="xw%d" % o, align_bytes=64) for o in range(PASSES)]
         w1s = [keep.tile([P, 2 * PASSES, H], U8, name="w1s%d" % pair, align_bytes=64) for pair in range(2)]
         w2s = keep.tile([P, E, N], U8, name="w2s", align_bytes=64)
-        w1w = {}
+        first_words_at = 3 * KIB - C
+        w1w = [reuse.tile([P, PASSES, 2 * H], U8, name="w1w0", align_bytes=64, offset=first_words_at)]
+        w1w.extend(keep.tile([P, PASSES, 2 * H], U8, name="w1w%d" % e, align_bytes=64) for e in range(1, E))
         w2w = keep.tile([P, E, 2 * N], U8, name="w2w", align_bytes=64)
-        gate_sb = [keep.tile([P, SLOTS], F32, name="gate%d" % h) for h in range(HALVES)]
         placed = [keep.tile([P, T], F32, name="placed%d" % h) for h in range(HALVES)]
         ident = keep.tile([P, P], F32, name="ident")
         warm = keep.tile([P, 1], F32, name="warm")
+        gate_sb = [keep.tile([P, 2 * C], F32, name="gate%d" % pair) for pair in range(2)]
         zero = keep.tile([P, ZCOLS], F32, name="zero")
+        gs = {}
+        groups = [(0, 1), (1, 3), (3, 4)]
+        group_of = [0, 1, 1, 2]
+        moved = keep.tile([P, SLOTS], U8, name="moved", align_bytes=64)
+        for g, (first, end) in enumerate(groups):
+            gs[g, 1] = moved[:, first * C : end * C]
 
-        nc.gpsimd.memset(xs[:].rearrange("p o t -> p (o t)").bitcast(I32), 0)
-        nc.vector.memset(zero[:], 0.0)
+        first_cols_at = 0
+        rows_at = [(6 + 3 * e) * KIB for e in range(E)]
+        middle_words_at = 20 * KIB
+        LAP = 64
+
+        nc.gpsimd.memset(xs[:].bitcast(I32), 0)
+        nc.gpsimd.memset(zero[:], 0.0)
         nc.gpsimd.memset(w1s[0][:].rearrange("p g i -> p (g i)").bitcast(I32), 0)
+        nc.gpsimd.memset(moved[:].bitcast(I32), 0)
         nc.gpsimd.memset(w2s[:].rearrange("p e n -> p (e n)").bitcast(I32), 0)
         nc.gpsimd.memset(w1s[1][:].rearrange("p g i -> p (g i)").bitcast(I32), 0)
         make_identity(nc, ident[:])
 
-        def load_w1(first, end):
-            tile = keep.tile([P, (end - first) * PASSES, 2 * H], U8, name="w1w%d" % first, align_bytes=64)
-            nc.sync.dma_start(tile[:].bitcast(I32), w1_words[first:end].rearrange("e s p b -> p (e s) b").bitcast(I32))
-            for e in range(first, end):
-                for o in range(PASSES):
-                    w1w[e, o] = tile[:, (e - first) * PASSES + o, :]
+        def load_w1(e):
+            nc.sync.dma_start(w1w[e][:].bitcast(I32), w1_words[e].rearrange("s p b -> p s b").bitcast(I32))
 
-        def load_w1_scales(pair):
-            for q in range(4):
-                rows = w1_scales[2 * pair : 2 * pair + 2, :, 4 * q : 4 * q + 4, :]
-                nc.sync.dma_start(
-                    w1s[pair][32 * q : 32 * q + 4].bitcast(I32), rows.rearrange("e s f i -> f (e s) i").bitcast(I32)
-                )
+        def load_w1_scales(pair, first=0, end=4):
+            rows = w1_scales[2 * pair : 2 * pair + 2].rearrange("e s (q j) i -> j q (e s) i", j=4)
+            for j in range(first, end):
+                nc.sync.dma_start(w1s[pair][j:P:32].bitcast(I32), rows[j].bitcast(I32))
+
+        def gather_scales(pair):
+            first, end = groups[pair]
+            cols = offs_sb[:, first * LIST_COLS : end * LIST_COLS]
+            if pair == 2:
+                gs[pair, 0] = reuse.tile([P, C], U8, name="gs2_0", align_bytes=64, offset=first_words_at + C)
+            else:
+                gs[pair, 0] = keep.tile([P, (end - first) * C], U8, name="gs%d_0" % pair, align_bytes=64)
+            nc.vector.tensor_copy(gs[pair, 0][:], xs[:].indirect(cols))
+
+        def shift_scales(pair):
+            queue = nc.scalar if pair == 0 else nc.sync
+            queue.dma_start(gs[pair, 1][0 : P - SHIFT].bitcast(I32), gs[pair, 0][SHIFT:P].bitcast(I32))
 
         nc.sync.dma_start(offs_sb[:], offs)
-        nc.sync.dma_start(dst_sb[:], dst)
-        for q in range(4):
-            nc.sync.dma_start(
-                xs[32 * q : 32 * q + 4].bitcast(I32),
-                x_scales[:, 4 * q : 4 * q + 4, :].rearrange("o f t -> f o t").bitcast(I32),
-            )
-        nc.sync.dma_start(xw[:], x_words.rearrange("o p t r -> p o (t r)").bitcast(I32))
-        load_w1(0, 1)
-        load_w1_scales(0)
-        load_w1(1, 2)
+        x_rows = x_scales.rearrange("o (q j) t -> j q o t", j=4)
+        for j in range(4):
+            queue = nc.scalar if j >= 2 else nc.sync
+            queue.dma_start(xs[j:P:SHIFT].bitcast(I32), x_rows[j].bitcast(I32))
+        nc.sync.dma_start(xw[0][:], x_words[0].rearrange("p t r -> p (t r)").bitcast(I32))
+        load_w1_scales(0, 0, 3)
+        load_w1(0)
+        load_w1_scales(0, 3, 4)
+        nc.sync.dma_start(xw[1][:], x_words[1].rearrange("p t r -> p (t r)").bitcast(I32))
+        gather_scales(0)
+        shift_scales(0)
+        gather_scales(1)
+        load_w1(1)
+        shift_scales(1)
         nc.sync.dma_start(w2w[:].bitcast(I32), w2_words[:, 0].rearrange("e p b -> p e b").bitcast(I32))
-        for q in range(4):
-            nc.sync.dma_start(
-                w2s[32 * q : 32 * q + 4].bitcast(I32),
-                w2_scales[:, 0, 4 * q : 4 * q + 4, :].rearrange("e f n -> f e n").bitcast(I32),
-            )
-        nc.sync.dma_start(gate_sb[0][:], gate[0:P, :])
+        nc.sync.dma_start(gate_sb[0][:], gate[0:P, 0 : 2 * C])
+        load_w1(2)
+        nc.sync.dma_start(dst_sb[:], dst)
         load_w1_scales(1)
-        load_w1(2, 4)
-        nc.sync.dma_start(gate_sb[1][:], gate[P : 2 * P, :])
+        load_w1(3)
+        nc.sync.dma_start(gate_sb[1][:], gate[0:P, 2 * C : 4 * C])
 
         nc.scalar.activation(warm[:], zero[:, 0:1], GELU)
         for h in range(HALVES):
-            nc.scalar.copy(
-                placed[h][:].rearrange("p (r c) -> p r c", c=ZCOLS),
-                zero[:].unsqueeze(1).to_broadcast([P, T // ZCOLS, ZCOLS]),
-            )
+            for c0 in range(0, T, ZPIECE):
+                nc.scalar.copy(
+                    placed[h][:, c0 : c0 + ZPIECE].rearrange("p (r c) -> p r c", c=ZCOLS),
+                    zero[:].unsqueeze(1).to_broadcast([P, ZPIECE // ZCOLS, ZCOLS]),
+                )
+        w2_rows = w2_scales[:, 0].rearrange("e (q j) n -> j q e n", j=4)
+        for j in range(4):
+            nc.scalar.dma_start(w2s[j:P:32].bitcast(I32), w2_rows[j].bitcast(I32))
 
         gw = {}
-        gs = {}
+        acc = {}
+        h_rows = {}
         h_cols = {}
         y = {}
         ready = {}
-        H_BYTES = 2 * 4 * C
-        W_BYTES = 4 * C
-        follows_rows = {(1, 1): (2, 1), (2, 1): (3, 1)}
-        at_rows = {key: H_BYTES + i * W_BYTES for i, key in enumerate([(0, 0), (2, 1), (3, 1)])}
 
-        def gather_scales(pair, o):
-            cols = offs_sb[:, 2 * pair * LIST_COLS : 2 * (pair + 1) * LIST_COLS]
-            name = "gs%d_%d" % (pair, o)
-            if (pair, o) == (1, 1):
-                gs[pair, o] = reuse.tile([P, 2 * C], U8, name=name, align_bytes=64, offset=0)
-            elif (pair, o) == (1, 0):
-                gs[pair, o] = reuse.tile([P, 2 * C], U8, name=name, align_bytes=64, offset=at_rows[0, 0])
+        def gather_words(o, first, end, at=None, lead=0):
+            name = "gw%d_%d" % (o, first)
+            if at is None:
+                words = keep.tile([P, (end - first) * P], U32, name=name, align_bytes=64)
             else:
-                gs[pair, o] = keep.tile([P, 2 * C], U8, name=name, align_bytes=64)
-            nc.vector.tensor_copy(gs[pair, o][:], xs[:, o, :].indirect(cols))
+                words = reuse.tile([P, (end - first) * P], U32, name=name, align_bytes=64, offset=at)
+            cuts = [0, lead, (end - first) * P] if lead else [0, (end - first) * P]
+            for s0, s1 in zip(cuts[:-1], cuts[1:]):
+                cols = offs_sb[:, (first * P + s0) // 16 : (first * P + s1) // 16]
+                nc.vector.tensor_copy(words[:, s0:s1], xw[o][:].bitcast(U32).indirect(cols))
+            for block in range(first, end):
+                gw[o, block] = words[:, (block - first) * P : (block - first + 1) * P]
 
-        def gather_words(e, o):
-            cols = offs_sb[:, e * LIST_COLS : (e + 1) * LIST_COLS]
-            gw[e, o] = keep.tile([P, C], U32, name="gw%d_%d" % (e, o), align_bytes=64)
-            nc.vector.tensor_copy(gw[e, o][:], xw[:, o, :].bitcast(U32).indirect(cols))
-
-        acc = {}
-        h_rows = {}
-
-        def first_pass(e, c, o):
-            if o == 0:
-                acc[e, c] = psum_a.tile([P, H], F32, name="acc")
-            s0 = (e % 2) * C + c * P
+        def first_pass(e, c, o, bank, start, stop):
+            g = group_of[e]
+            s0 = (e - groups[g][0]) * C + c * P
             nc.tensor.matmul_mx(
-                out=acc[e, c][:],
-                lhsT=gw[e, o][:, c * P : (c + 1) * P].bitcast(FP8X4),
-                lhsT_scale=gs[e // 2, o][:, s0 : s0 + P],
-                rhs=w1w[e, o].bitcast(FP4X4),
+                out=bank[:],
+                lhsT=gw[o, 2 * e + c].bitcast(FP8X4),
+                lhsT_scale=gs[g, o][:, s0 : s0 + P],
+                rhs=w1w[e][:, o, :].bitcast(FP4X4),
                 rhs_scale=w1s[e // 2][:, (e % 2) * PASSES + o, :],
-                start=(o == 0),
-                stop=(o == PASSES - 1),
+                start=start,
+                stop=stop,
             )
-            if o == PASSES - 1:
-                if (e, c) in at_rows:
-                    name = "h_rows%d_%d" % (e, c)
-                    rows = reuse.tile([P, 2, P, 2], BF16, name=name, align_bytes=64, offset=at_rows[e, c])
-                else:
-                    rows = work.tile([P, 2, P, 2], BF16, name="h_rows", bufs=4)
-                nc.scalar.activation(rows[:], acc[e, c][:].rearrange("s (p u d) -> s u p d", u=2, d=2), GELU)
-                h_rows[e, c] = rows
 
         def first_product(e, c):
+            acc[e, c] = psum.tile([P, H], F32, name="acc_first" if (e, c) == (0, 0) else "acc%d" % c)
             for o in range(PASSES):
-                first_pass(e, c, o)
+                first_pass(e, c, o, acc[e, c], o == 0, o == PASSES - 1)
 
-        def turn(e):
-            turned = psum_t.tile([P, 2, C], F32, name="turned")
-            for c in range(C // P):
-                h_pairs = h_rows[e, c][:].rearrange("s u p d -> s (u p d)").bitcast(F32)
+        def gelu(e, c):
+            sums = acc[e, c][:].rearrange("s (p u d) -> s u p d", u=2, d=2)
+            name = "h_rows%d_%d" % (e, c)
+            if (e, c) in ((0, 1), (1, 0)):
                 for u in range(2):
-                    nc.tensor.transpose(turned[:, u, c * P : (c + 1) * P], h_pairs[:, u * P : (u + 1) * P], ident[:])
-            if e == 0:
-                h_cols[e] = reuse.tile([P, 4 * C], BF16, name="h_cols_first", align_bytes=64, offset=0)
+                    if u == 0:
+                        half = keep.tile([P, P, 2], BF16, name=name + "a", align_bytes=64)
+                    else:
+                        half = reuse.tile([P, P, 2], BF16, name=name + "b", align_bytes=64, offset=rows_at[0])
+                    nc.scalar.activation(half[:], sums[:, u], GELU)
+                    h_rows[e, c, u] = half[:].rearrange("s p d -> s (p d)").bitcast(F32)
+                return
+            if c == 1:
+                rows = reuse.tile([P, 2, P, 2], BF16, name=name, align_bytes=64, offset=rows_at[e])
+            elif e > 0:
+                rows = reuse.tile([P, 2, P, 2], BF16, name=name, align_bytes=64, offset=rows_at[e - 1] + LAP - KIB)
             else:
-                h_cols[e] = keep.tile([P, 4 * C], BF16, name="h_cols%d" % e, align_bytes=64)
-            nc.scalar.copy(
-                h_cols[e][:].bitcast(F32).rearrange("p (s u) -> p s u", u=2), turned[:].rearrange("p u s -> p s u")
-            )
+                rows = keep.tile([P, 2, P, 2], BF16, name=name, align_bytes=64)
+            nc.scalar.activation(rows[:], sums, GELU)
+            pairs = rows[:].rearrange("s u p d -> s (u p d)").bitcast(F32)
+            for u in range(2):
+                h_rows[e, c, u] = pairs[:, u * P : (u + 1) * P]
 
-        def second_layer(e):
-            codes = work.tile([P, C], U32, name="codes", align_bytes=64)
-            h_scales = work.tile([P, C], U8, name="h_scales", align_bytes=64)
-            nc.vector.quantize_mx(out=codes[:].bitcast(FP8X4), scales=h_scales[:], in_=h_cols[e][:])
-            y[e] = psum_y.tile([P, HALVES, C], F32, name="y")
-            for h in range(HALVES):
-                nc.tensor.matmul_mx(
-                    out=y[e][:, h, :],
-                    lhsT=w2w[:, e, 2 * h * P : 2 * (h + 1) * P].bitcast(FP4X4),
-                    lhsT_scale=w2s[:, e, h * P : (h + 1) * P],
-                    rhs=codes[:].bitcast(FP8X4),
-                    rhs_scale=h_scales[:],
-                    start=True,
-                    stop=True,
+        def turn(e, c):
+            turned = psum.tile([P, 2, P], F32, name="turned%d" % c)
+            for u in range(2):
+                nc.tensor.transpose(turned[:, u, :], h_rows[e, c, u], ident[:])
+            if c == 0 and e == 0:
+                h_cols[e] = reuse.tile([P, 4 * C], BF16, name="h_cols0", align_bytes=64, offset=first_cols_at)
+            elif c == 0:
+                h_cols[e] = keep.tile([P, 4 * C], BF16, name="h_cols%d" % e, align_bytes=64)
+            words = h_cols[e][:, 4 * c * P : 4 * (c + 1) * P].bitcast(F32)
+            nc.scalar.copy(words.rearrange("p (s u) -> p s u", u=2), turned[:].rearrange("p u s -> p s u"))
+
+        def second_layer(e, width):
+            codes = keep.tile([P, C], U32, name="codes%d" % e, align_bytes=64)
+            if e == 1:
+                h_scales = reuse.tile([P, C], U8, name="h_scales1", align_bytes=64, offset=middle_words_at)
+            else:
+                h_scales = keep.tile([P, C], U8, name="h_scales%d" % e, align_bytes=64)
+            for s0 in range(0, C, width):
+                nc.vector.quantize_mx(
+                    out=codes[:, s0 : s0 + width].bitcast(FP8X4),
+                    scales=h_scales[:, s0 : s0 + width],
+                    in_=h_cols[e][:, 4 * s0 : 4 * (s0 + width)],
                 )
+            for h in range(HALVES):
+                bank = psum.tile([P, C], F32, name="y%d" % h)
+                y[e, h, 0] = bank[:]
+                for s0 in range(0, C, width):
+                    sums = bank[:, s0 : s0 + width]
+                    if (e, h) == (0, 0):
+                        if s0 == 0:
+                            early = psum.tile([P, P], F32, name="early")
+                            sums = early[:]
+                        y[e, h, s0] = sums
+                    nc.tensor.matmul_mx(
+                        out=sums,
+                        lhsT=w2w[:, e, 2 * h * P : 2 * (h + 1) * P].bitcast(FP4X4),
+                        lhsT_scale=w2s[:, e, h * P : (h + 1) * P],
+                        rhs=codes[:, s0 : s0 + width].bitcast(FP8X4),
+                        rhs_scale=h_scales[:, s0 : s0 + width],
+                        start=True,
+                        stop=True,
+                    )
 
         def empty_y(e, h):
             name = "ready%d_%d" % (e, h)
-            if (e, h) in follows_rows:
-                ready[e, h] = reuse.tile([P, C], F32, name=name, align_bytes=64, offset=at_rows[follows_rows[e, h]])
+            if (e, h) == (0, 1):
+                ready[e, h] = reuse.tile([P, C], F32, name=name, align_bytes=64, offset=middle_words_at + C)
+            elif h == 1 and e + 1 < E:
+                ready[e, h] = reuse.tile([P, C], F32, name=name, align_bytes=64, offset=rows_at[e + 1] + LAP)
             else:
                 ready[e, h] = keep.tile([P, C], F32, name=name, align_bytes=64)
-            nc.scalar.copy(ready[e, h][:], y[e][:, h, :])
+            width = P if (e, h) == (0, 0) else C
+            for s0 in range(0, C, width):
+                nc.scalar.copy(ready[e, h][:, s0 : s0 + width], y[e, h, s0])
 
         def scatter(e, h):
             cols = dst_sb[:, e * LIST_COLS : (e + 1) * LIST_COLS]
-            nc.vector.tensor_tensor(
-                placed[h][:].indirect(cols), ready[e, h][:], gate_sb[h][:, e * C : (e + 1) * C], MULT
-            )
+            weights = gate_sb[e // 2][:, (e % 2) * C : (e % 2 + 1) * C]
+            nc.vector.tensor_tensor(placed[h][:].indirect(cols), ready[e, h][:], weights, MULT)
 
-        gather_scales(0, 0)
-        gather_scales(0, 1)
+        gather_words(0, 0, 2)
+        gather_words(1, 0, 3, lead=T // 8)
+        gather_words(0, 2, 4)
+        gather_words(1, 3, 5, middle_words_at)
+        gather_words(1, 5, 8)
         for e in range(E):
-            for o in range(PASSES):
-                gather_words(e, o)
-        first_product(0, 0)
-        first_product(0, 1)
-        first_product(1, 0)
-        turn(0)
-        gather_scales(1, 0)
-        first_product(1, 1)
-        turn(1)
-        second_layer(0)
-        gather_scales(1, 1)
-        empty_y(0, 0)
-        empty_y(0, 1)
-        first_product(2, 0)
-        second_layer(1)
-        empty_y(1, 0)
-        first_product(2, 1)
-        first_product(3, 0)
-        first_product(3, 1)
-        turn(2)
-        empty_y(1, 1)
-        second_layer(2)
-        turn(3)
-        empty_y(2, 0)
-        empty_y(2, 1)
-        second_layer(3)
-        empty_y(3, 0)
-        empty_y(3, 1)
-        for e in range(E):
-            for h in range(HALVES):
-                scatter(e, h)
+            for c in range(2):
+                if (e, c) != (2, 0):
+                    first_product(e, c)
+                gelu(e, c)
+            if e == 0:
+                gather_scales(2)
+                shift_scales(2)
+                gather_words(0, 4, 6, first_words_at + 2 * C)
+            turn(e, 0)
+            turn(e, 1)
+            if e == 1:
+                first_product(2, 0)
+            if e > 0:
+                empty_y(e - 1, 1)
+            second_layer(e, P if e == 0 else C)
+            if e == 0:
+                gather_words(0, 6, 8, first_cols_at)
+            else:
+                scatter(e - 1, 1)
+            empty_y(e, 0)
+            scatter(e, 0)
+        empty_y(E - 1, 1)
+        scatter(E - 1, 1)
+
         for h in range(HALVES):
             nc.sync.dma_start(out[h * P : (h + 1) * P, :], placed[h][:])

@@ -49,7 +49,6 @@ def tile_moe_two_mlp_gelu_kernel(
         w2w = keep.tile([P, E, 2 * N], U8, name="w2w", align_bytes=64)
         placed = [keep.tile([P, T], F32, name="placed%d" % h) for h in range(HALVES)]
         ident = keep.tile([P, P], F32, name="ident")
-        warm = keep.tile([P, 1], F32, name="warm")
         gate_sb = [keep.tile([P, 2 * C], F32, name="gate%d" % pair) for pair in range(2)]
         zero = keep.tile([P, ZCOLS], F32, name="zero")
         gs = {}
@@ -116,12 +115,12 @@ def tile_moe_two_mlp_gelu_kernel(
         load_w1(3)
         nc.sync.dma_start(gate_sb[1][:], gate[0:P, 2 * C : 4 * C])
 
-        nc.scalar.activation(warm[:], zero[:, 0:1], GELU)
         for h in range(HALVES):
             for c0 in range(0, T, ZPIECE):
-                nc.scalar.copy(
+                nc.scalar.activation(
                     placed[h][:, c0 : c0 + ZPIECE].rearrange("p (r c) -> p r c", c=ZCOLS),
                     zero[:].unsqueeze(1).to_broadcast([P, ZPIECE // ZCOLS, ZCOLS]),
+                    GELU,
                 )
         w2_rows = w2_scales[:, 0].rearrange("e (q j) n -> j q e n", j=4)
         for j in range(4):

@@ -24,7 +24,7 @@ LIST_COLS = C // 16
 HALVES = N // P
 SHIFT = 16
 ZCOLS = 16
-ZPIECE = 640
+ZFIRST = 896
 KIB = 1024
 
 
@@ -98,9 +98,9 @@ def tile_moe_two_mlp_gelu_kernel(
             queue = nc.scalar if j >= 2 else nc.sync
             queue.dma_start(xs[j:P:SHIFT].bitcast(I32), x_rows[j].bitcast(I32))
         nc.sync.dma_start(xw[0][:], x_words[0].rearrange("p t r -> p (t r)").bitcast(I32))
-        load_w1_scales(0, 0, 3)
+        load_w1_scales(0, 0, 1)
         load_w1(0)
-        load_w1_scales(0, 3, 4)
+        load_w1_scales(0, 1, 4)
         nc.sync.dma_start(xw[1][:], x_words[1].rearrange("p t r -> p (t r)").bitcast(I32))
         gather_scales(0)
         shift_scales(0)
@@ -116,10 +116,11 @@ def tile_moe_two_mlp_gelu_kernel(
         nc.sync.dma_start(gate_sb[1][:], gate[0:P, 2 * C : 4 * C])
 
         for h in range(HALVES):
-            for c0 in range(0, T, ZPIECE):
+            cut = ZFIRST if h == 0 else T // 2
+            for c0, c1 in ((0, cut), (cut, T)):
                 nc.scalar.activation(
-                    placed[h][:, c0 : c0 + ZPIECE].rearrange("p (r c) -> p r c", c=ZCOLS),
-                    zero[:].unsqueeze(1).to_broadcast([P, ZPIECE // ZCOLS, ZCOLS]),
+                    placed[h][:, c0:c1].rearrange("p (r c) -> p r c", c=ZCOLS),
+                    zero[:].unsqueeze(1).to_broadcast([P, (c1 - c0) // ZCOLS, ZCOLS]),
                     GELU,
                 )
         w2_rows = w2_scales[:, 0].rearrange("e (q j) n -> j q e n", j=4)
@@ -133,13 +134,13 @@ def tile_moe_two_mlp_gelu_kernel(
         y = {}
         ready = {}
 
-        def gather_words(o, first, end, at=None, lead=0):
+        def gather_words(o, first, end, at=None, leads=()):
             name = "gw%d_%d" % (o, first)
             if at is None:
                 words = keep.tile([P, (end - first) * P], U32, name=name, align_bytes=64)
             else:
                 words = reuse.tile([P, (end - first) * P], U32, name=name, align_bytes=64, offset=at)
-            cuts = [0, lead, (end - first) * P] if lead else [0, (end - first) * P]
+            cuts = [0] + list(leads) + [(end - first) * P]
             for s0, s1 in zip(cuts[:-1], cuts[1:]):
                 cols = offs_sb[:, (first * P + s0) // 16 : (first * P + s1) // 16]
                 nc.vector.tensor_copy(words[:, s0:s1], xw[o][:].bitcast(U32).indirect(cols))
@@ -195,8 +196,13 @@ def tile_moe_two_mlp_gelu_kernel(
                 h_cols[e] = reuse.tile([P, 4 * C], BF16, name="h_cols0", align_bytes=64, offset=first_cols_at)
             elif c == 0:
                 h_cols[e] = keep.tile([P, 4 * C], BF16, name="h_cols%d" % e, align_bytes=64)
-            words = h_cols[e][:, 4 * c * P : 4 * (c + 1) * P].bitcast(F32)
-            nc.scalar.copy(words.rearrange("p (s u) -> p s u", u=2), turned[:].rearrange("p u s -> p s u"))
+            step = P // 2 if (e, c) == (0, 1) else P
+            for s0 in range(0, P, step):
+                words = h_cols[e][:, 4 * (c * P + s0) : 4 * (c * P + s0 + step)].bitcast(F32)
+                nc.scalar.copy(
+                    words.rearrange("p (s u) -> p s u", u=2),
+                    turned[:, :, s0 : s0 + step].rearrange("p u s -> p s u"),
+                )
 
         def second_layer(e, width):
             codes = keep.tile([P, C], U32, name="codes%d" % e, align_bytes=64)
@@ -204,11 +210,12 @@ def tile_moe_two_mlp_gelu_kernel(
                 h_scales = reuse.tile([P, C], U8, name="h_scales1", align_bytes=64, offset=middle_words_at)
             else:
                 h_scales = keep.tile([P, C], U8, name="h_scales%d" % e, align_bytes=64)
-            for s0 in range(0, C, width):
+            cuts = [0, P, P + P // 2, C] if e == 0 else [0, C]
+            for s0, s1 in zip(cuts[:-1], cuts[1:]):
                 nc.vector.quantize_mx(
-                    out=codes[:, s0 : s0 + width].bitcast(FP8X4),
-                    scales=h_scales[:, s0 : s0 + width],
-                    in_=h_cols[e][:, 4 * s0 : 4 * (s0 + width)],
+                    out=codes[:, s0:s1].bitcast(FP8X4),
+                    scales=h_scales[:, s0:s1],
+                    in_=h_cols[e][:, 4 * s0 : 4 * s1],
                 )
             for h in range(HALVES):
                 bank = psum.tile([P, C], F32, name="y%d" % h)
@@ -247,9 +254,8 @@ def tile_moe_two_mlp_gelu_kernel(
             weights = gate_sb[e // 2][:, (e % 2) * C : (e % 2 + 1) * C]
             nc.vector.tensor_tensor(placed[h][:].indirect(cols), ready[e, h][:], weights, MULT)
 
-        gather_words(0, 0, 2)
-        gather_words(1, 0, 3, lead=T // 8)
-        gather_words(0, 2, 4)
+        gather_words(0, 0, 4, leads=(T // 8, T // 4))
+        gather_words(1, 0, 3, leads=(T // 8,))
         gather_words(1, 3, 5, middle_words_at)
         gather_words(1, 5, 8)
         for e in range(E):

@@ -68,7 +68,9 @@ def tile_moe_two_mlp_gelu_kernel(
         nc.gpsimd.memset(w1s[0][:].rearrange("p g i -> p (g i)").bitcast(I32), 0)
         nc.gpsimd.memset(moved[:].bitcast(I32), 0)
         nc.gpsimd.memset(w2s[:].rearrange("p e n -> p (e n)").bitcast(I32), 0)
-        nc.gpsimd.memset(w1s[1][:].rearrange("p g i -> p (g i)").bitcast(I32), 0)
+        nc.vector.tensor_copy(
+            w1s[1][:].rearrange("p g i -> p (g i)").bitcast(I32), w1s[0][:].rearrange("p g i -> p (g i)").bitcast(I32)
+        )
         make_identity(nc, ident[:])
 
         def load_w1(e):
@@ -204,7 +206,7 @@ def tile_moe_two_mlp_gelu_kernel(
                     turned[:, :, s0 : s0 + step].rearrange("p u s -> p s u"),
                 )
 
-        def second_layer(e, width):
+        def second_layer(e):
             codes = keep.tile([P, C], U32, name="codes%d" % e, align_bytes=64)
             if e == 1:
                 h_scales = reuse.tile([P, C], U8, name="h_scales1", align_bytes=64, offset=middle_words_at)
@@ -220,6 +222,7 @@ def tile_moe_two_mlp_gelu_kernel(
             for h in range(HALVES):
                 bank = psum.tile([P, C], F32, name="y%d" % h)
                 y[e, h, 0] = bank[:]
+                width = P if (e, h) == (0, 0) else C
                 for s0 in range(0, C, width):
                     sums = bank[:, s0 : s0 + width]
                     if (e, h) == (0, 0):
@@ -273,7 +276,7 @@ def tile_moe_two_mlp_gelu_kernel(
                 first_product(2, 0)
             if e > 0:
                 empty_y(e - 1, 1)
-            second_layer(e, P if e == 0 else C)
+            second_layer(e)
             if e == 0:
                 gather_words(0, 6, 8, first_cols_at)
             else:

@@ -15,6 +15,7 @@ U8 = mybir.dt.uint8
 FP8X4 = mybir.dt.float8_e4m3fn_x4
 FP4X4 = mybir.dt.float4_e2m1fn_x4
 GELU = mybir.ActivationFunctionType.Gelu_apprx_tanh
+COPY = mybir.ActivationFunctionType.Copy
 MULT = mybir.AluOpType.mult
 
 P = 128
@@ -37,72 +38,83 @@ def tile_moe_two_mlp_gelu_kernel(
         reuse = ctx.enter_context(tc.tile_pool(name="reuse", bufs=1))
         psum = ctx.enter_context(tc.psum_pool(name="psum", bufs=1))
 
+        LAP = 64
+        at_half = KIB
+        at_rows = {(1, 1): at_half + KIB // 2 - LAP}
+        at_rows[2, 1] = at_rows[1, 1] + KIB - LAP
+        at_words0_7 = at_rows[1, 1] + 2 * LAP
+        at_halves = {(0, 1): at_half, (1, 0): at_half - KIB // 2 + LAP}
+        at_words1_1 = 6 * KIB
+        at_words1_5 = at_words1_1 + KIB - LAP
+        at_cols0 = 10 * KIB
+        at_cols1 = 20 * KIB
+        at_words1_0 = 16 * KIB
+        at_words0_3 = at_words1_0 + KIB // 2 - LAP
+
+        def sb(shape, dtype, name, at=None):
+            if at is None:
+                return keep.tile(shape, dtype, name=name, align_bytes=64)
+            return reuse.tile(shape, dtype, name=name, align_bytes=64, offset=at)
+
         offs_sb = keep.tile([P, SLOTS // 16], U16, name="offs_sb")
         dst_sb = keep.tile([P, SLOTS // 16], U16, name="dst_sb")
-        xs = keep.tile([P, T], U8, name="xs", align_bytes=64)
-        xw = [keep.tile([P, T], I32, name="xw%d" % o, align_bytes=64) for o in range(PASSES)]
-        w1s = [keep.tile([P, 2 * PASSES, H], U8, name="w1s%d" % pair, align_bytes=64) for pair in range(2)]
-        w2s = keep.tile([P, E, N], U8, name="w2s", align_bytes=64)
-        first_words_at = 3 * KIB - C
-        w1w = [reuse.tile([P, PASSES, 2 * H], U8, name="w1w0", align_bytes=64, offset=first_words_at)]
-        w1w.extend(keep.tile([P, PASSES, 2 * H], U8, name="w1w%d" % e, align_bytes=64) for e in range(1, E))
-        w2w = keep.tile([P, E, 2 * N], U8, name="w2w", align_bytes=64)
+        xs = sb([P, T], U8, "xs")
+        xw = [sb([P, T], I32, "xw%d" % o) for o in range(PASSES)]
+        w1s = [sb([P, 2 * PASSES, H], U8, "w1s%d" % pair) for pair in range(2)]
+        w2s = sb([P, E, N], U8, "w2s")
+        w1w = [sb([P, PASSES, 2 * H], U8, "w1w%d" % e) for e in range(E)]
+        w2w = sb([P, E, 2 * N], U8, "w2w")
         placed = [keep.tile([P, T], F32, name="placed%d" % h) for h in range(HALVES)]
         ident = keep.tile([P, P], F32, name="ident")
-        gate_sb = [keep.tile([P, 2 * C], F32, name="gate%d" % pair) for pair in range(2)]
+        gate_sb = [sb([P, 2 * C], F32, "gate%d" % pair) for pair in range(2)]
         zero = keep.tile([P, ZCOLS], F32, name="zero")
         gs = {}
-        groups = [(0, 1), (1, 3), (3, 4)]
-        group_of = [0, 1, 1, 2]
-        moved = keep.tile([P, SLOTS], U8, name="moved", align_bytes=64)
+        groups = [(0, 2), (2, 4)]
+        group_of = [0, 0, 1, 1]
+        moved = sb([P, SLOTS], U8, "moved")
         for g, (first, end) in enumerate(groups):
             gs[g, 1] = moved[:, first * C : end * C]
-
-        first_cols_at = 0
-        rows_at = [(6 + 3 * e) * KIB for e in range(E)]
-        middle_words_at = 20 * KIB
-        LAP = 64
 
         nc.gpsimd.memset(xs[:].bitcast(I32), 0)
         nc.gpsimd.memset(zero[:], 0.0)
         nc.gpsimd.memset(w1s[0][:].rearrange("p g i -> p (g i)").bitcast(I32), 0)
-        nc.gpsimd.memset(moved[:].bitcast(I32), 0)
-        nc.gpsimd.memset(w2s[:].rearrange("p e n -> p (e n)").bitcast(I32), 0)
         nc.vector.tensor_copy(
             w1s[1][:].rearrange("p g i -> p (g i)").bitcast(I32), w1s[0][:].rearrange("p g i -> p (g i)").bitcast(I32)
         )
+        nc.vector.tensor_copy(
+            w2s[:].rearrange("p e n -> p (e n)").bitcast(I32), w1s[0][:, 0:2, :].rearrange("p g i -> p (g i)").bitcast(I32)
+        )
+        nc.gpsimd.memset(moved[:].bitcast(I32), 0)
         make_identity(nc, ident[:])
 
         def load_w1(e):
             nc.sync.dma_start(w1w[e][:].bitcast(I32), w1_words[e].rearrange("s p b -> p s b").bitcast(I32))
 
-        def load_w1_scales(pair, first=0, end=4):
+        def load_w1_scales(pair, first, end, queue):
             rows = w1_scales[2 * pair : 2 * pair + 2].rearrange("e s (q j) i -> j q (e s) i", j=4)
             for j in range(first, end):
-                nc.sync.dma_start(w1s[pair][j:P:32].bitcast(I32), rows[j].bitcast(I32))
+                queue.dma_start(w1s[pair][j:P:32].bitcast(I32), rows[j].bitcast(I32))
 
-        def gather_scales(pair):
-            first, end = groups[pair]
+        def gather_scales(g):
+            first, end = groups[g]
             cols = offs_sb[:, first * LIST_COLS : end * LIST_COLS]
-            if pair == 2:
-                gs[pair, 0] = reuse.tile([P, C], U8, name="gs2_0", align_bytes=64, offset=first_words_at + C)
-            else:
-                gs[pair, 0] = keep.tile([P, (end - first) * C], U8, name="gs%d_0" % pair, align_bytes=64)
-            nc.vector.tensor_copy(gs[pair, 0][:], xs[:].indirect(cols))
+            gs[g, 0] = sb([P, (end - first) * C], U8, "gs%d_0" % g)
+            nc.vector.tensor_copy(gs[g, 0][:], xs[:].indirect(cols))
 
-        def shift_scales(pair):
-            queue = nc.scalar if pair == 0 else nc.sync
-            queue.dma_start(gs[pair, 1][0 : P - SHIFT].bitcast(I32), gs[pair, 0][SHIFT:P].bitcast(I32))
+        def shift_scales(g):
+            queue = nc.scalar if g == 0 else nc.sync
+            queue.dma_start(gs[g, 1][0 : P - SHIFT].bitcast(I32), gs[g, 0][SHIFT:P].bitcast(I32))
 
         nc.sync.dma_start(offs_sb[:], offs)
+        load_w1_scales(1, 0, 2, nc.gpsimd)
         x_rows = x_scales.rearrange("o (q j) t -> j q o t", j=4)
         for j in range(4):
             queue = nc.scalar if j >= 2 else nc.sync
             queue.dma_start(xs[j:P:SHIFT].bitcast(I32), x_rows[j].bitcast(I32))
         nc.sync.dma_start(xw[0][:], x_words[0].rearrange("p t r -> p (t r)").bitcast(I32))
-        load_w1_scales(0, 0, 1)
+        load_w1_scales(0, 0, 1, nc.sync)
         load_w1(0)
-        load_w1_scales(0, 1, 4)
+        load_w1_scales(0, 1, 4, nc.sync)
         nc.sync.dma_start(xw[1][:], x_words[1].rearrange("p t r -> p (t r)").bitcast(I32))
         gather_scales(0)
         shift_scales(0)
@@ -110,12 +122,12 @@ def tile_moe_two_mlp_gelu_kernel(
         load_w1(1)
         shift_scales(1)
         nc.sync.dma_start(w2w[:].bitcast(I32), w2_words[:, 0].rearrange("e p b -> p e b").bitcast(I32))
-        nc.sync.dma_start(gate_sb[0][:], gate[0:P, 0 : 2 * C])
+        load_w1_scales(1, 2, 4, nc.sync)
         load_w1(2)
-        nc.sync.dma_start(dst_sb[:], dst)
-        load_w1_scales(1)
         load_w1(3)
-        nc.sync.dma_start(gate_sb[1][:], gate[0:P, 2 * C : 4 * C])
+        nc.sync.dma_start(dst_sb[:], dst)
+        nc.sync.dma_start(gate_sb[0][:], gate[0:P, 0 : 2 * C])
+        nc.sync.dma_start(gate_sb[1][:], gate[0:P, 2 * C :])
 
         for h in range(HALVES):
             cut = ZFIRST if h == 0 else T // 2
@@ -131,17 +143,17 @@ def tile_moe_two_mlp_gelu_kernel(
 
         gw = {}
         acc = {}
+        acc_bank = [0, 1, 2, 1, 3, 1, 3, 0]
         h_rows = {}
         h_cols = {}
+        turned = {}
+        codes = {}
+        h_scales = {}
         y = {}
         ready = {}
 
         def gather_words(o, first, end, at=None, leads=()):
-            name = "gw%d_%d" % (o, first)
-            if at is None:
-                words = keep.tile([P, (end - first) * P], U32, name=name, align_bytes=64)
-            else:
-                words = reuse.tile([P, (end - first) * P], U32, name=name, align_bytes=64, offset=at)
+            words = sb([P, (end - first) * P], U32, "gw%d_%d" % (o, first), at)
             cuts = [0] + list(leads) + [(end - first) * P]
             for s0, s1 in zip(cuts[:-1], cuts[1:]):
                 cols = offs_sb[:, (first * P + s0) // 16 : (first * P + s1) // 16]
@@ -149,142 +161,163 @@ def tile_moe_two_mlp_gelu_kernel(
             for block in range(first, end):
                 gw[o, block] = words[:, (block - first) * P : (block - first + 1) * P]
 
-        def first_pass(e, c, o, bank, start, stop):
+        def first_pass(e, c, o):
             g = group_of[e]
             s0 = (e - groups[g][0]) * C + c * P
+            if o == 0:
+                acc[e, c] = psum.tile([P, H], F32, name="acc%d" % acc_bank[2 * e + c])
             nc.tensor.matmul_mx(
-                out=bank[:],
+                out=acc[e, c][:],
                 lhsT=gw[o, 2 * e + c].bitcast(FP8X4),
                 lhsT_scale=gs[g, o][:, s0 : s0 + P],
                 rhs=w1w[e][:, o, :].bitcast(FP4X4),
                 rhs_scale=w1s[e // 2][:, (e % 2) * PASSES + o, :],
-                start=start,
-                stop=stop,
+                start=o == 0,
+                stop=o == PASSES - 1,
             )
 
         def first_product(e, c):
-            acc[e, c] = psum.tile([P, H], F32, name="acc_first" if (e, c) == (0, 0) else "acc%d" % c)
             for o in range(PASSES):
-                first_pass(e, c, o, acc[e, c], o == 0, o == PASSES - 1)
+                first_pass(e, c, o)
 
         def gelu(e, c):
             sums = acc[e, c][:].rearrange("s (p u d) -> s u p d", u=2, d=2)
-            name = "h_rows%d_%d" % (e, c)
-            if (e, c) in ((0, 1), (1, 0)):
-                for u in range(2):
-                    if u == 0:
-                        half = keep.tile([P, P, 2], BF16, name=name + "a", align_bytes=64)
-                    else:
-                        half = reuse.tile([P, P, 2], BF16, name=name + "b", align_bytes=64, offset=rows_at[0])
-                    nc.scalar.activation(half[:], sums[:, u], GELU)
-                    h_rows[e, c, u] = half[:].rearrange("s p d -> s (p d)").bitcast(F32)
-                return
-            if c == 1:
-                rows = reuse.tile([P, 2, P, 2], BF16, name=name, align_bytes=64, offset=rows_at[e])
-            elif e > 0:
-                rows = reuse.tile([P, 2, P, 2], BF16, name=name, align_bytes=64, offset=rows_at[e - 1] + LAP - KIB)
-            else:
-                rows = keep.tile([P, 2, P, 2], BF16, name=name, align_bytes=64)
+            rows = sb([P, 2, P, 2], BF16, "h_rows%d_%d" % (e, c), at_rows.get((e, c)))
             nc.scalar.activation(rows[:], sums, GELU)
             pairs = rows[:].rearrange("s u p d -> s (u p d)").bitcast(F32)
             for u in range(2):
                 h_rows[e, c, u] = pairs[:, u * P : (u + 1) * P]
 
-        def turn(e, c):
-            turned = psum.tile([P, 2, P], F32, name="turned%d" % c)
-            for u in range(2):
-                nc.tensor.transpose(turned[:, u, :], h_rows[e, c, u], ident[:])
-            if c == 0 and e == 0:
-                h_cols[e] = reuse.tile([P, 4 * C], BF16, name="h_cols0", align_bytes=64, offset=first_cols_at)
-            elif c == 0:
-                h_cols[e] = keep.tile([P, 4 * C], BF16, name="h_cols%d" % e, align_bytes=64)
-            step = P // 2 if (e, c) == (0, 1) else P
-            for s0 in range(0, P, step):
-                words = h_cols[e][:, 4 * (c * P + s0) : 4 * (c * P + s0 + step)].bitcast(F32)
-                nc.scalar.copy(
-                    words.rearrange("p (s u) -> p s u", u=2),
-                    turned[:, :, s0 : s0 + step].rearrange("p u s -> p s u"),
-                )
+        def gelu_half(e, c, u):
+            sums = acc[e, c][:].rearrange("s (p u d) -> s u p d", u=2, d=2)
+            half = sb([P, P, 2], BF16, "h_rows%d_%d_%d" % (e, c, u), at_halves[e, c] if u == 1 else None)
+            nc.scalar.activation(half[:], sums[:, u], GELU)
+            h_rows[e, c, u] = half[:].rearrange("s p d -> s (p d)").bitcast(F32)
 
-        def second_layer(e):
-            codes = keep.tile([P, C], U32, name="codes%d" % e, align_bytes=64)
-            if e == 1:
-                h_scales = reuse.tile([P, C], U8, name="h_scales1", align_bytes=64, offset=middle_words_at)
-            else:
-                h_scales = keep.tile([P, C], U8, name="h_scales%d" % e, align_bytes=64)
-            cuts = [0, P, P + P // 2, C] if e == 0 else [0, C]
+        def turn(e, first, end, bank):
+            turned[e] = psum.tile([P, end - first, 2, P], F32, name=bank)
+            for c in range(first, end):
+                for u in range(2):
+                    nc.tensor.transpose(turned[e][:, c - first, u, :], h_rows[e, c, u], ident[:])
+            if first == 0:
+                h_cols[e] = sb([P, 4 * C], BF16, "h_cols%d" % e, {0: at_cols0, 1: at_cols1}.get(e))
+
+        def empty_turned(e, first, end):
+            words = h_cols[e][:, 4 * first * P : 4 * end * P].bitcast(F32)
+            nc.scalar.copy(
+                words.rearrange("p (c s u) -> p c s u", u=2, s=P),
+                turned[e][:].rearrange("p c u s -> p c s u"),
+            )
+
+        def empty_turned_part(e, c, s0, s1):
+            words = h_cols[e][:, 4 * (c * P + s0) : 4 * (c * P + s1)].bitcast(F32)
+            nc.scalar.copy(
+                words.rearrange("p (s u) -> p s u", u=2),
+                turned[e][:, 0, :, s0:s1].rearrange("p u s -> p s u"),
+            )
+
+        def quantise(e, cuts=(0, C)):
+            codes[e] = sb([P, C], U32, "codes%d" % e)
+            h_scales[e] = sb([P, C], U8, "h_scales%d" % e)
             for s0, s1 in zip(cuts[:-1], cuts[1:]):
                 nc.vector.quantize_mx(
-                    out=codes[:, s0:s1].bitcast(FP8X4),
-                    scales=h_scales[:, s0:s1],
+                    out=codes[e][:, s0:s1].bitcast(FP8X4),
+                    scales=h_scales[e][:, s0:s1],
                     in_=h_cols[e][:, 4 * s0 : 4 * s1],
                 )
-            for h in range(HALVES):
-                bank = psum.tile([P, C], F32, name="y%d" % h)
-                y[e, h, 0] = bank[:]
-                width = P if (e, h) == (0, 0) else C
-                for s0 in range(0, C, width):
-                    sums = bank[:, s0 : s0 + width]
-                    if (e, h) == (0, 0):
-                        if s0 == 0:
-                            early = psum.tile([P, P], F32, name="early")
-                            sums = early[:]
-                        y[e, h, s0] = sums
-                    nc.tensor.matmul_mx(
-                        out=sums,
-                        lhsT=w2w[:, e, 2 * h * P : 2 * (h + 1) * P].bitcast(FP4X4),
-                        lhsT_scale=w2s[:, e, h * P : (h + 1) * P],
-                        rhs=codes[:, s0 : s0 + width].bitcast(FP8X4),
-                        rhs_scale=h_scales[:, s0 : s0 + width],
-                        start=True,
-                        stop=True,
-                    )
 
-        def empty_y(e, h):
-            name = "ready%d_%d" % (e, h)
-            if (e, h) == (0, 1):
-                ready[e, h] = reuse.tile([P, C], F32, name=name, align_bytes=64, offset=middle_words_at + C)
-            elif h == 1 and e + 1 < E:
-                ready[e, h] = reuse.tile([P, C], F32, name=name, align_bytes=64, offset=rows_at[e + 1] + LAP)
-            else:
-                ready[e, h] = keep.tile([P, C], F32, name=name, align_bytes=64)
-            width = P if (e, h) == (0, 0) else C
-            for s0 in range(0, C, width):
-                nc.scalar.copy(ready[e, h][:, s0 : s0 + width], y[e, h, s0])
+        def second_product(e, first, end, bank):
+            sums = psum.tile([P, end - first, C], F32, name=bank)
+            y[e] = sums
+            for h in range(first, end):
+                nc.tensor.matmul_mx(
+                    out=sums[:, h - first, :],
+                    lhsT=w2w[:, e, 2 * h * P : 2 * (h + 1) * P].bitcast(FP4X4),
+                    lhsT_scale=w2s[:, e, h * P : (h + 1) * P],
+                    rhs=codes[e][:].bitcast(FP8X4),
+                    rhs_scale=h_scales[e][:],
+                    start=True,
+                    stop=True,
+                )
 
-        def scatter(e, h):
+        high = sb([P, SLOTS], F32, "high", at_cols1)
+        low = sb([P, 2 * C], F32, "low")
+
+        def gate_of(e):
+            return gate_sb[e // 2][:, (e % 2) * C : (e % 2 + 1) * C]
+
+        def weigh(e, h):
+            values = high[:, e * C : (e + 1) * C] if h == 1 else low[:, (e - 2) * C : (e - 1) * C]
+            nc.vector.tensor_tensor(values, y[e][:, h, :], gate_of(e), MULT)
+
+        def empty_low(e):
+            ready[e] = sb([P, C], F32, "ready%d" % e)
+            nc.scalar.copy(ready[e][:], y[e][:, 0, :])
+
+        def scatter_weighing(e):
             cols = dst_sb[:, e * LIST_COLS : (e + 1) * LIST_COLS]
-            weights = gate_sb[e // 2][:, (e % 2) * C : (e % 2 + 1) * C]
-            nc.vector.tensor_tensor(placed[h][:].indirect(cols), ready[e, h][:], weights, MULT)
+            nc.vector.tensor_tensor(placed[0][:].indirect(cols), ready[e][:], gate_of(e), MULT)
 
-        gather_words(0, 0, 4, leads=(T // 8, T // 4))
-        gather_words(1, 0, 3, leads=(T // 8,))
-        gather_words(1, 3, 5, middle_words_at)
-        gather_words(1, 5, 8)
-        for e in range(E):
+        gather_words(0, 0, 3, leads=(P, 2 * P))
+        gather_words(1, 0, 1, at_words1_0)
+        gather_words(1, 1, 3, at_words1_1)
+        gather_words(1, 3, 5)
+        for o in range(PASSES):
             for c in range(2):
-                if (e, c) != (2, 0):
-                    first_product(e, c)
-                gelu(e, c)
-            if e == 0:
-                gather_scales(2)
-                shift_scales(2)
-                gather_words(0, 4, 6, first_words_at + 2 * C)
-            turn(e, 0)
-            turn(e, 1)
-            if e == 1:
-                first_product(2, 0)
-            if e > 0:
-                empty_y(e - 1, 1)
-            second_layer(e)
-            if e == 0:
-                gather_words(0, 6, 8, first_cols_at)
-            else:
-                scatter(e - 1, 1)
-            empty_y(e, 0)
-            scatter(e, 0)
-        empty_y(E - 1, 1)
-        scatter(E - 1, 1)
+                first_pass(0, c, o)
+        first_product(1, 0)
+        gather_words(0, 3, 6, at_words0_3)
+        gather_words(1, 5, 8, at_words1_5)
+        gelu(0, 0)
+        gelu_half(0, 1, 0)
+        gelu_half(0, 1, 1)
+        turn(0, 0, 1, "x0")
+        empty_turned(0, 0, 1)
+        gelu_half(1, 0, 0)
+        turn(0, 1, 2, "x2")
+        empty_turned_part(0, 1, 0, P // 2)
+        empty_turned_part(0, 1, P // 2, P)
+        first_product(1, 1)
+        gelu_half(1, 0, 1)
+        first_product(2, 0)
+        gelu(1, 1)
+        quantise(0, (0, P, P + P // 2, C))
+        gather_words(0, 6, 7, at_cols0)
+        second_product(0, 0, 2, "x1")
+        gelu(2, 0)
+        empty_low(0)
+        turn(1, 0, 2, "x0")
+        gather_words(0, 7, 8, at_words0_7)
+        first_product(2, 1)
+        empty_turned(1, 0, 2)
+        scatter_weighing(0)
+        first_product(3, 0)
+        first_product(3, 1)
+        gelu(2, 1)
+        gelu(3, 0)
+        gelu(3, 1)
+        quantise(1, (0, P, C))
+        weigh(0, 1)
+        turn(2, 0, 2, "x2")
+        second_product(1, 0, 2, "x3")
+        empty_turned(2, 0, 2)
+        empty_low(1)
+        quantise(2)
+        weigh(1, 1)
+        turn(3, 0, 2, "x0")
+        empty_turned(3, 0, 2)
+        second_product(2, 0, 2, "x0")
+        scatter_weighing(1)
+        quantise(3)
+        second_product(3, 0, 2, "x2")
+        for e in (2, 3):
+            weigh(e, 1)
+            weigh(e, 0)
+        nc.vector.tensor_copy(placed[0][:].indirect(dst_sb[:, 2 * LIST_COLS :]), low[:])
+        cuts = (0, 3 * P, 6 * P, SLOTS)
+        for s0, s1 in zip(cuts[:-1], cuts[1:]):
+            nc.scalar.activation(placed[1][:].indirect(dst_sb[:, s0 // 16 : s1 // 16]), high[:, s0:s1], COPY)
 
         for h in range(HALVES):
-            nc.sync.dma_start(out[h * P : (h + 1) * P, :], placed[h][:])
+            queue = nc.sync if h == 0 else nc.scalar
+            queue.dma_start(out[h * P : (h + 1) * P, :], placed[h][:])

@@ -39,15 +39,16 @@ def tile_moe_two_mlp_gelu_kernel(
         psum = ctx.enter_context(tc.psum_pool(name="psum", bufs=1))
 
         LAP = 64
-        at_half = KIB
+        at_half = 6 * KIB
         at_rows = {(1, 1): at_half + KIB // 2 - LAP}
         at_rows[2, 1] = at_rows[1, 1] + KIB - LAP
         at_words0_7 = at_rows[1, 1] + 2 * LAP
         at_halves = {(0, 1): at_half, (1, 0): at_half - KIB // 2 + LAP}
-        at_words1_1 = 6 * KIB
+        at_ready0 = 30 * KIB
+        at_high = at_ready0 + LAP - 4 * KIB
+        at_words1_1 = 12 * KIB
         at_words1_5 = at_words1_1 + KIB - LAP
-        at_cols0 = 10 * KIB
-        at_cols1 = 20 * KIB
+        at_cols0 = 20 * KIB
         at_words1_0 = 16 * KIB
         at_words0_3 = at_words1_0 + KIB // 2 - LAP
 
@@ -200,7 +201,7 @@ def tile_moe_two_mlp_gelu_kernel(
                 for u in range(2):
                     nc.tensor.transpose(turned[e][:, c - first, u, :], h_rows[e, c, u], ident[:])
             if first == 0:
-                h_cols[e] = sb([P, 4 * C], BF16, "h_cols%d" % e, {0: at_cols0, 1: at_cols1}.get(e))
+                h_cols[e] = sb([P, 4 * C], BF16, "h_cols%d" % e, at_cols0 if e == 0 else None)
 
         def empty_turned(e, first, end):
             words = h_cols[e][:, 4 * first * P : 4 * end * P].bitcast(F32)
@@ -240,7 +241,7 @@ def tile_moe_two_mlp_gelu_kernel(
                     stop=True,
                 )
 
-        high = sb([P, SLOTS], F32, "high", at_cols1)
+        high = sb([P, SLOTS], F32, "high", at_high)
         low = sb([P, 2 * C], F32, "low")
 
         def gate_of(e):
@@ -251,7 +252,7 @@ def tile_moe_two_mlp_gelu_kernel(
             nc.vector.tensor_tensor(values, y[e][:, h, :], gate_of(e), MULT)
 
         def empty_low(e):
-            ready[e] = sb([P, C], F32, "ready%d" % e)
+            ready[e] = sb([P, C], F32, "ready%d" % e, at_ready0 if e == 0 else None)
             nc.scalar.copy(ready[e][:], y[e][:, 0, :])
 
         def scatter_weighing(e):
@@ -290,34 +291,35 @@ def tile_moe_two_mlp_gelu_kernel(
         gather_words(0, 7, 8, at_words0_7)
         first_product(2, 1)
         empty_turned(1, 0, 2)
+        quantise(1)
         scatter_weighing(0)
+        second_product(1, 0, 2, "x3")
         first_product(3, 0)
         first_product(3, 1)
         gelu(2, 1)
+        empty_low(1)
         gelu(3, 0)
         gelu(3, 1)
-        quantise(1, (0, P, C))
         weigh(0, 1)
-        turn(2, 0, 2, "x2")
-        second_product(1, 0, 2, "x3")
-        empty_turned(2, 0, 2)
-        empty_low(1)
-        quantise(2)
         weigh(1, 1)
-        turn(3, 0, 2, "x0")
-        empty_turned(3, 0, 2)
-        second_product(2, 0, 2, "x0")
         scatter_weighing(1)
+        turn(2, 0, 2, "x2")
+        empty_turned(2, 0, 2)
+        quantise(2)
+        turn(3, 0, 1, "x0")
+        empty_turned(3, 0, 1)
+        turn(3, 1, 2, "x1")
+        empty_turned(3, 1, 2)
+        second_product(2, 0, 2, "x1")
         quantise(3)
         second_product(3, 0, 2, "x2")
         for e in (2, 3):
-            weigh(e, 1)
-            weigh(e, 0)
+            weigh(e, 3 - e)
+            weigh(e, e - 2)
         nc.vector.tensor_copy(placed[0][:].indirect(dst_sb[:, 2 * LIST_COLS :]), low[:])
         cuts = (0, 3 * P, 6 * P, SLOTS)
         for s0, s1 in zip(cuts[:-1], cuts[1:]):
             nc.scalar.activation(placed[1][:].indirect(dst_sb[:, s0 // 16 : s1 // 16]), high[:, s0:s1], COPY)
 
         for h in range(HALVES):
-            queue = nc.sync if h == 0 else nc.scalar
-            queue.dma_start(out[h * P : (h + 1) * P, :], placed[h][:])
+            nc.sync.dma_start(out[h * P : (h + 1) * P, :], placed[h][:])

@@ -107,7 +107,6 @@ def tile_moe_two_mlp_gelu_kernel(
             queue.dma_start(gs[g, 1][0 : P - SHIFT].bitcast(I32), gs[g, 0][SHIFT:P].bitcast(I32))
 
         nc.sync.dma_start(offs_sb[:], offs)
-        load_w1_scales(1, 0, 2, nc.gpsimd)
         x_rows = x_scales.rearrange("o (q j) t -> j q o t", j=4)
         for j in range(4):
             queue = nc.scalar if j >= 2 else nc.sync
@@ -138,6 +137,7 @@ def tile_moe_two_mlp_gelu_kernel(
                     zero[:].unsqueeze(1).to_broadcast([P, (c1 - c0) // ZCOLS, ZCOLS]),
                     GELU,
                 )
+        load_w1_scales(1, 0, 2, nc.scalar)
         w2_rows = w2_scales[:, 0].rearrange("e (q j) n -> j q e n", j=4)
         for j in range(4):
             nc.scalar.dma_start(w2s[j:P:32].bitcast(I32), w2_rows[j].bitcast(I32))
@@ -253,7 +253,10 @@ def tile_moe_two_mlp_gelu_kernel(
 
         def empty_low(e):
             ready[e] = sb([P, C], F32, "ready%d" % e, at_ready0 if e == 0 else None)
-            nc.scalar.copy(ready[e][:], y[e][:, 0, :])
+            if e == 0:
+                nc.vector.tensor_copy(ready[e][:], y[e][:, 0, :])
+            else:
+                nc.scalar.copy(ready[e][:], y[e][:, 0, :])
 
         def scatter_weighing(e):
             cols = dst_sb[:, e * LIST_COLS : (e + 1) * LIST_COLS]
@@ -308,9 +311,9 @@ def tile_moe_two_mlp_gelu_kernel(
         quantise(2)
         turn(3, 0, 1, "x0")
         empty_turned(3, 0, 1)
-        turn(3, 1, 2, "x1")
+        turn(3, 1, 2, "acc2")
         empty_turned(3, 1, 2)
-        second_product(2, 0, 2, "x1")
+        second_product(2, 0, 2, "acc2")
         quantise(3)
         second_product(3, 0, 2, "x2")
         for e in (2, 3):

from contextlib import ExitStack

import concourse.mybir as mybir
from concourse.masks import make_identity

K, T, E, C, H, N = 1024, 1280, 4, 256, 512, 256
FLOPS = 2 * E * C * (K * H + H * N)

F32 = mybir.dt.float32
BF16 = mybir.dt.bfloat16
I32 = mybir.dt.int32
U32 = mybir.dt.uint32
U16 = mybir.dt.uint16
U8 = mybir.dt.uint8
FP8X4 = mybir.dt.float8_e4m3fn_x4
FP4X4 = mybir.dt.float4_e2m1fn_x4
GELU = mybir.ActivationFunctionType.Gelu_apprx_tanh
COPY = mybir.ActivationFunctionType.Copy
MULT = mybir.AluOpType.mult

P = 128
PASSES = K // 512
SLOTS = E * C
LIST_COLS = C // 16
HALVES = N // P
SHIFT = 16
ZCOLS = 16
ZFIRST = 896
KIB = 1024


def tile_moe_two_mlp_gelu_kernel(
    tc, x_words, x_scales, w1_words, w1_scales, w2_words, w2_scales, gate, offs, dst, out
):
    nc = tc.nc
    with ExitStack() as ctx:
        keep = ctx.enter_context(tc.tile_pool(name="keep", bufs=1))
        reuse = ctx.enter_context(tc.tile_pool(name="reuse", bufs=1))
        psum = ctx.enter_context(tc.psum_pool(name="psum", bufs=1))

        LAP = 64
        at_half = 6 * KIB
        at_rows = {(1, 1): at_half + KIB // 2 - LAP}
        at_rows[2, 1] = at_rows[1, 1] + KIB - LAP
        at_words0_7 = at_rows[1, 1] + 2 * LAP
        at_halves = {(0, 1): at_half, (1, 0): at_half - KIB // 2 + LAP}
        at_ready0 = 30 * KIB
        at_high = at_ready0 + LAP - 4 * KIB
        at_words1_1 = 12 * KIB
        at_words1_5 = at_words1_1 + KIB - LAP
        at_cols0 = 20 * KIB
        at_words1_0 = 16 * KIB
        at_words0_3 = at_words1_0 + KIB // 2 - LAP

        def sb(shape, dtype, name, at=None):
            if at is None:
                return keep.tile(shape, dtype, name=name, align_bytes=64)
            return reuse.tile(shape, dtype, name=name, align_bytes=64, offset=at)

        offs_sb = keep.tile([P, SLOTS // 16], U16, name="offs_sb")
        dst_sb = keep.tile([P, SLOTS // 16], U16, name="dst_sb")
        xs = sb([P, T], U8, "xs")
        xw = [sb([P, T], I32, "xw%d" % o) for o in range(PASSES)]
        w1s = [sb([P, 2 * PASSES, H], U8, "w1s%d" % pair) for pair in range(2)]
        w2s = sb([P, E, N], U8, "w2s")
        w1w = [sb([P, PASSES, 2 * H], U8, "w1w%d" % e) for e in range(E)]
        w2w = sb([P, E, 2 * N], U8, "w2w")
        placed = [keep.tile([P, T], F32, name="placed%d" % h) for h in range(HALVES)]
        ident = keep.tile([P, P], F32, name="ident")
        gate_sb = [sb([P, 2 * C], F32, "gate%d" % pair) for pair in range(2)]
        zero = keep.tile([P, ZCOLS], F32, name="zero")
        gs = {}
        groups = [(0, 2), (2, 4)]
        group_of = [0, 0, 1, 1]
        moved = sb([P, SLOTS], U8, "moved")
        for g, (first, end) in enumerate(groups):
            gs[g, 1] = moved[:, first * C : end * C]

        nc.gpsimd.memset(xs[:].bitcast(I32), 0)
        nc.gpsimd.memset(zero[:], 0.0)
        nc.gpsimd.memset(w1s[0][:].rearrange("p g i -> p (g i)").bitcast(I32), 0)
        nc.vector.tensor_copy(
            w1s[1][:].rearrange("p g i -> p (g i)").bitcast(I32), w1s[0][:].rearrange("p g i -> p (g i)").bitcast(I32)
        )
        nc.vector.tensor_copy(
            w2s[:].rearrange("p e n -> p (e n)").bitcast(I32), w1s[0][:, 0:2, :].rearrange("p g i -> p (g i)").bitcast(I32)
        )
        nc.gpsimd.memset(moved[:].bitcast(I32), 0)
        make_identity(nc, ident[:])

        def load_w1(e):
            nc.sync.dma_start(w1w[e][:].bitcast(I32), w1_words[e].rearrange("s p b -> p s b").bitcast(I32))

        def load_w1_scales(pair, first, end, queue):
            rows = w1_scales[2 * pair : 2 * pair + 2].rearrange("e s (q j) i -> j q (e s) i", j=4)
            for j in range(first, end):
                queue.dma_start(w1s[pair][j:P:32].bitcast(I32), rows[j].bitcast(I32))

        def gather_scales(g):
            first, end = groups[g]
            cols = offs_sb[:, first * LIST_COLS : end * LIST_COLS]
            gs[g, 0] = sb([P, (end - first) * C], U8, "gs%d_0" % g)
            nc.vector.tensor_copy(gs[g, 0][:], xs[:].indirect(cols))

        def shift_scales(g):
            queue = nc.scalar if g == 0 else nc.sync
            queue.dma_start(gs[g, 1][0 : P - SHIFT].bitcast(I32), gs[g, 0][SHIFT:P].bitcast(I32))

        nc.sync.dma_start(offs_sb[:], offs)
        x_rows = x_scales.rearrange("o (q j) t -> j q o t", j=4)
        for j in range(4):
            queue = nc.scalar if j >= 2 else nc.sync
            queue.dma_start(xs[j:P:SHIFT].bitcast(I32), x_rows[j].bitcast(I32))
        nc.sync.dma_start(xw[0][:], x_words[0].rearrange("p t r -> p (t r)").bitcast(I32))
        load_w1_scales(0, 0, 1, nc.sync)
        load_w1(0)
        load_w1_scales(0, 1, 4, nc.sync)
        nc.sync.dma_start(xw[1][:], x_words[1].rearrange("p t r -> p (t r)").bitcast(I32))
        gather_scales(0)
        shift_scales(0)
        gather_scales(1)
        load_w1(1)
        shift_scales(1)
        nc.sync.dma_start(w2w[:].bitcast(I32), w2_words[:, 0].rearrange("e p b -> p e b").bitcast(I32))
        load_w1_scales(1, 2, 4, nc.sync)
        load_w1(2)
        load_w1(3)
        nc.sync.dma_start(dst_sb[:], dst)
        nc.sync.dma_start(gate_sb[0][:], gate[0:P, 0 : 2 * C])
        nc.sync.dma_start(gate_sb[1][:], gate[0:P, 2 * C :])

        for h in range(HALVES):
            cut = ZFIRST if h == 0 else T // 2
            for c0, c1 in ((0, cut), (cut, T)):
                nc.scalar.activation(
                    placed[h][:, c0:c1].rearrange("p (r c) -> p r c", c=ZCOLS),
                    zero[:].unsqueeze(1).to_broadcast([P, (c1 - c0) // ZCOLS, ZCOLS]),
                    GELU,
                )
        load_w1_scales(1, 0, 2, nc.scalar)
        w2_rows = w2_scales[:, 0].rearrange("e (q j) n -> j q e n", j=4)
        for j in range(4):
            nc.scalar.dma_start(w2s[j:P:32].bitcast(I32), w2_rows[j].bitcast(I32))

        gw = {}
        acc = {}
        acc_bank = [0, 1, 2, 1, 3, 1, 3, 0]
        h_rows = {}
        h_cols = {}
        turned = {}
        codes = {}
        h_scales = {}
        y = {}
        ready = {}

        def gather_words(o, first, end, at=None, leads=()):
            words = sb([P, (end - first) * P], U32, "gw%d_%d" % (o, first), at)
            cuts = [0] + list(leads) + [(end - first) * P]
            for s0, s1 in zip(cuts[:-1], cuts[1:]):
                cols = offs_sb[:, (first * P + s0) // 16 : (first * P + s1) // 16]
                nc.vector.tensor_copy(words[:, s0:s1], xw[o][:].bitcast(U32).indirect(cols))
            for block in range(first, end):
                gw[o, block] = words[:, (block - first) * P : (block - first + 1) * P]

        def first_pass(e, c, o):
            g = group_of[e]
            s0 = (e - groups[g][0]) * C + c * P
            if o == 0:
                acc[e, c] = psum.tile([P, H], F32, name="acc%d" % acc_bank[2 * e + c])
            nc.tensor.matmul_mx(
                out=acc[e, c][:],
                lhsT=gw[o, 2 * e + c].bitcast(FP8X4),
                lhsT_scale=gs[g, o][:, s0 : s0 + P],
                rhs=w1w[e][:, o, :].bitcast(FP4X4),
                rhs_scale=w1s[e // 2][:, (e % 2) * PASSES + o, :],
                start=o == 0,
                stop=o == PASSES - 1,
            )

        def first_product(e, c):
            for o in range(PASSES):
                first_pass(e, c, o)

        def gelu(e, c):
            sums = acc[e, c][:].rearrange("s (p u d) -> s u p d", u=2, d=2)
            rows = sb([P, 2, P, 2], BF16, "h_rows%d_%d" % (e, c), at_rows.get((e, c)))
            nc.scalar.activation(rows[:], sums, GELU)
            pairs = rows[:].rearrange("s u p d -> s (u p d)").bitcast(F32)
            for u in range(2):
                h_rows[e, c, u] = pairs[:, u * P : (u + 1) * P]

        def gelu_half(e, c, u):
            sums = acc[e, c][:].rearrange("s (p u d) -> s u p d", u=2, d=2)
            half = sb([P, P, 2], BF16, "h_rows%d_%d_%d" % (e, c, u), at_halves[e, c] if u == 1 else None)
            nc.scalar.activation(half[:], sums[:, u], GELU)
            h_rows[e, c, u] = half[:].rearrange("s p d -> s (p d)").bitcast(F32)

        def turn(e, first, end, bank):
            turned[e] = psum.tile([P, end - first, 2, P], F32, name=bank)
            for c in range(first, end):
                for u in range(2):
                    nc.tensor.transpose(turned[e][:, c - first, u, :], h_rows[e, c, u], ident[:])
            if first == 0:
                h_cols[e] = sb([P, 4 * C], BF16, "h_cols%d" % e, at_cols0 if e == 0 else None)

        def empty_turned(e, first, end):
            words = h_cols[e][:, 4 * first * P : 4 * end * P].bitcast(F32)
            nc.scalar.copy(
                words.rearrange("p (c s u) -> p c s u", u=2, s=P),
                turned[e][:].rearrange("p c u s -> p c s u"),
            )

        def empty_turned_part(e, c, s0, s1):
            words = h_cols[e][:, 4 * (c * P + s0) : 4 * (c * P + s1)].bitcast(F32)
            nc.scalar.copy(
                words.rearrange("p (s u) -> p s u", u=2),
                turned[e][:, 0, :, s0:s1].rearrange("p u s -> p s u"),
            )

        def quantise(e, cuts=(0, C)):
            codes[e] = sb([P, C], U32, "codes%d" % e)
            h_scales[e] = sb([P, C], U8, "h_scales%d" % e)
            for s0, s1 in zip(cuts[:-1], cuts[1:]):
                nc.vector.quantize_mx(
                    out=codes[e][:, s0:s1].bitcast(FP8X4),
                    scales=h_scales[e][:, s0:s1],
                    in_=h_cols[e][:, 4 * s0 : 4 * s1],
                )

        def second_product(e, first, end, bank):
            sums = psum.tile([P, end - first, C], F32, name=bank)
            y[e] = sums
            for h in range(first, end):
                nc.tensor.matmul_mx(
                    out=sums[:, h - first, :],
                    lhsT=w2w[:, e, 2 * h * P : 2 * (h + 1) * P].bitcast(FP4X4),
                    lhsT_scale=w2s[:, e, h * P : (h + 1) * P],
                    rhs=codes[e][:].bitcast(FP8X4),
                    rhs_scale=h_scales[e][:],
                    start=True,
                    stop=True,
                )

        high = sb([P, SLOTS], F32, "high", at_high)
        low = sb([P, 2 * C], F32, "low")

        def gate_of(e):
            return gate_sb[e // 2][:, (e % 2) * C : (e % 2 + 1) * C]

        def weigh(e, h):
            values = high[:, e * C : (e + 1) * C] if h == 1 else low[:, (e - 2) * C : (e - 1) * C]
            nc.vector.tensor_tensor(values, y[e][:, h, :], gate_of(e), MULT)

        def empty_low(e):
            ready[e] = sb([P, C], F32, "ready%d" % e, at_ready0 if e == 0 else None)
            if e == 0:
                nc.vector.tensor_copy(ready[e][:], y[e][:, 0, :])
            else:
                nc.scalar.copy(ready[e][:], y[e][:, 0, :])

        def scatter_weighing(e):
            cols = dst_sb[:, e * LIST_COLS : (e + 1) * LIST_COLS]
            nc.vector.tensor_tensor(placed[0][:].indirect(cols), ready[e][:], gate_of(e), MULT)

        gather_words(0, 0, 3, leads=(P, 2 * P))
        gather_words(1, 0, 1, at_words1_0)
        gather_words(1, 1, 3, at_words1_1)
        gather_words(1, 3, 5)
        for o in range(PASSES):
            for c in range(2):
                first_pass(0, c, o)
        first_product(1, 0)
        gather_words(0, 3, 6, at_words0_3)
        gather_words(1, 5, 8, at_words1_5)
        gelu(0, 0)
        gelu_half(0, 1, 0)
        gelu_half(0, 1, 1)
        turn(0, 0, 1, "x0")
        empty_turned(0, 0, 1)
        gelu_half(1, 0, 0)
        turn(0, 1, 2, "x2")
        empty_turned_part(0, 1, 0, P // 2)
        empty_turned_part(0, 1, P // 2, P)
        first_product(1, 1)
        gelu_half(1, 0, 1)
        first_product(2, 0)
        gelu(1, 1)
        quantise(0, (0, P, P + P // 2, C))
        gather_words(0, 6, 7, at_cols0)
        second_product(0, 0, 2, "x1")
        gelu(2, 0)
        empty_low(0)
        turn(1, 0, 2, "x0")
        gather_words(0, 7, 8, at_words0_7)
        first_product(2, 1)
        empty_turned(1, 0, 2)
        quantise(1)
        scatter_weighing(0)
        second_product(1, 0, 2, "x3")
        first_product(3, 0)
        first_product(3, 1)
        gelu(2, 1)
        empty_low(1)
        gelu(3, 0)
        gelu(3, 1)
        weigh(0, 1)
        weigh(1, 1)
        scatter_weighing(1)
        turn(2, 0, 2, "x2")
        empty_turned(2, 0, 2)
        quantise(2)
        turn(3, 0, 1, "x0")
        empty_turned(3, 0, 1)
        turn(3, 1, 2, "acc2")
        empty_turned(3, 1, 2)
        second_product(2, 0, 2, "acc2")
        quantise(3)
        second_product(3, 0, 2, "x2")
        for e in (2, 3):
            weigh(e, 3 - e)
            weigh(e, e - 2)
        nc.vector.tensor_copy(placed[0][:].indirect(dst_sb[:, 2 * LIST_COLS :]), low[:])
        cuts = (0, 3 * P, 6 * P, SLOTS)
        for s0, s1 in zip(cuts[:-1], cuts[1:]):
            nc.scalar.activation(placed[1][:].indirect(dst_sb[:, s0 // 16 : s1 // 16]), high[:, s0:s1], COPY)

        for h in range(HALVES):
            nc.sync.dma_start(out[h * P : (h + 1) * P, :], placed[h][:])
